import numpy as np
import ml_dtypes


def mxq(x, axis, fmt="e4m3"):
    dtype, down = {"e4m3": (ml_dtypes.float8_e4m3fn, 7), "e5m2": (ml_dtypes.float8_e5m2, 14)}[fmt]
    v = np.moveaxis(np.asarray(x, np.float32).astype(ml_dtypes.bfloat16).astype(np.float64), axis, -1)
    blocks = v.reshape(v.shape[:-1] + (-1, 32))
    amax = np.abs(blocks).max(-1, keepdims=True)
    byte = np.maximum(np.where(amax > 0, np.frexp(amax)[1] - 1 + 127, 0) - down, 1)
    scale = np.exp2(byte - 127.0)
    codes = (blocks / scale).astype(np.float32).astype(dtype).astype(np.float64)
    return np.moveaxis((codes * scale).reshape(v.shape), -1, axis)


WIDE = False


def mx_kscale(k):
    if not WIDE:
        return np.ones(k)
    levels = np.array([24, -24, 12, -12, 0])
    if k % 512:
        return np.exp2(np.random.permutation(np.resize(levels, k // 32))).repeat(32)
    a = np.empty((k // 512, 16))
    for p in range(k // 512):
        a[p, :8] = np.random.permutation(np.resize(levels, 8))
        for g in range(8):
            far = levels[np.abs(levels - a[p, g]) >= 10]
            a[p, g + 8] = far[np.random.randint(len(far))]
    return np.exp2(a.ravel()).repeat(32)


def f64(x):
    return np.asarray(x).astype(np.float64)


def striped8(idx):
    return np.concatenate([v.reshape(-1, 16).T for v in idx]).astype(np.uint16)


def unstriped8(offs):
    return np.stack([offs[16 * g:16 * g + 16].T.reshape(-1) for g in range(8)]).astype(np.int64)


E2M1 = np.array([0.0, 0.5, 1.0, 1.5, 2.0, 3.0, 4.0, 6.0, -0.0, -0.5, -1.0, -1.5, -2.0, -3.0, -4.0, -6.0])


def pack_weight(w, fmt):
    k, n = w.shape
    w = f64(np.asarray(w, np.float32).astype(ml_dtypes.bfloat16)).reshape(k // 32, 32, n)
    amax = np.abs(w).max(1)
    if fmt == "e4m3":
        byte = np.frexp(amax)[1] - 1 + 127 - 7
    else:
        mant, ex = np.frexp(amax / 6.0)
        byte = np.where(mant > 0.5, ex, ex - 1) + 127
    byte = np.clip(np.where(amax > 0, byte, 1), 1, 254)
    scaled = (w * np.exp2(127.0 - byte)[:, None, :]).reshape(k, n).astype(np.float32)
    by_word = np.ascontiguousarray(scaled.reshape(k // 512, 128, 4, n).transpose(0, 1, 3, 2))
    if fmt == "e4m3":
        words = by_word.astype(ml_dtypes.float8_e4m3fn).view(np.uint8)
    else:
        c = by_word.astype(ml_dtypes.float4_e2m1fn).view(np.uint8) & 0xF
        words = (c[..., 0::2] | (c[..., 1::2] << 4)).reshape(k // 512, 128, 2 * n)
    return np.ascontiguousarray(words), np.ascontiguousarray(byte.astype(np.uint8).reshape(k // 512, 16, n))


def unpack_weight(words, scales, fmt):
    g, _, n = scales.shape
    words = np.ascontiguousarray(words).reshape(g, 128, n, -1)
    if fmt == "e4m3":
        vals = words.view(ml_dtypes.float8_e4m3fn).astype(np.float64)
    else:
        nib = np.empty((g, 128, n, 4), np.uint8)
        nib[..., 0::2] = words & 0xF
        nib[..., 1::2] = words >> 4
        vals = E2M1[nib]
    vals = vals * np.repeat(np.exp2(scales.astype(np.float64) - 127.0), 8, axis=1)[..., None]
    return vals.transpose(0, 1, 3, 2).reshape(g * 512, n)


def planes(y):
    n, m = y.shape
    v = y.astype(np.float32).astype(ml_dtypes.bfloat16).astype(np.float64).reshape(n // 32, 32, m)
    top = np.abs(v).max(1)
    byte = np.clip(np.where(top > 0, np.frexp(top)[1] - 1 + 127 - 7, 1), 1, 254)
    codes = (v * np.exp2(127.0 - byte)[:, None, :]).reshape(n, m).astype(np.float32).astype(ml_dtypes.float8_e4m3fn).view(np.uint8)
    words = codes.reshape(n // 512, 128, 4, m).transpose(0, 1, 3, 2)
    return np.ascontiguousarray(words), np.ascontiguousarray(byte.astype(np.uint8).reshape(n // 512, 16, m))


def sigm(f):
    return 1.0 / (1.0 + np.exp(-np.maximum(f, -700.0)))


K, R, N, T, J = 512, 512, 512, 2048, 1024


def setup_inputs():
    n = np.random.standard_normal
    s = mx_kscale(K)[:, None]
    u = mx_kscale(R)[:, None]
    p_wg = pack_weight(n((K, R)) / np.sqrt(K) / s, "e2m1")
    p_wu = pack_weight(n((K, R)) / np.sqrt(K) / s * u.T, "e4m3")
    p_wd = pack_weight(n((R, N)) / np.sqrt(R) / u, "e4m3")
    return {
        "xT": (n((K, T)) * s).astype(np.float32),
        "wgt": np.repeat(np.random.uniform(0.5, 2.0, (8, J)), 16, axis=0).astype(np.float32),
        "wg_words": p_wg[0],
        "wg_scales": p_wg[1],
        "wu_words": p_wu[0],
        "wu_scales": p_wu[1],
        "wd_words": p_wd[0],
        "wd_scales": p_wd[1],
        "g": (n((N, J))).astype(np.float32),
        "offs": striped8(np.stack([np.random.permutation(T)[:J] for _ in range(8)])),
    }


def reference(xT, wgt, wg_words, wg_scales, wu_words, wu_scales, wd_words, wd_scales, g, offs):
    idx = unstriped8(offs)
    rows = np.arange(K)
    xg = f64(wgt)[rows // 4 % 128] * f64(xT)[rows[:, None], idx[rows % 512 // 64]]
    xT_ = mxq(xg, 0, "e4m3")
    wg_ = unpack_weight(wg_words, wg_scales, "e2m1")
    wu_ = unpack_weight(wu_words, wu_scales, "e4m3")
    ga = wg_.T @ xT_
    ub = wu_.T @ xT_
    h = sigm(ga) * ub
    h_ = mxq(h, 0, "e4m3")
    wd_ = unpack_weight(wd_words, wd_scales, "e4m3")
    y = wd_.T @ h_
    out_0 = y * f64(g)
    return (out_0,) + planes(out_0)

@@ -1,0 +1,217 @@
+from contextlib import ExitStack
+
+import concourse.mybir as mybir
+
+K, R, N, T, J = 512, 512, 512, 2048, 1024
+FLOPS = 2 * J * (2 * K * R + R * N)
+
+F32 = mybir.dt.float32
+BF16 = mybir.dt.bfloat16
+I32 = mybir.dt.int32
+U32 = mybir.dt.uint32
+U16 = mybir.dt.uint16
+U8 = mybir.dt.uint8
+FP8X4 = mybir.dt.float8_e4m3fn_x4
+FP4X4 = mybir.dt.float4_e2m1fn_x4
+MULT = mybir.AluOpType.mult
+SIGMOID = mybir.ActivationFunctionType.Sigmoid
+
+P = 128
+PACK = 4
+C = 128
+CHUNKS = J // C
+LANES = 16
+FIRST = 256
+PLANE_AT = (0, 8 * C, 10 * C, 18 * C)
+LOAD_ORDER = (0, 2, 3, 1)
+GATE_CUTS = ((0, 256), (256, 512), (512, 1024))
+
+
+def tile_list_sigm_mulP_kernel(
+    tc, xT, wgt, wg_words, wg_scales, wu_words, wu_scales, wd_words, wd_scales, g, offs, out_0, out_1, out_2
+):
+    nc = tc.nc
+    with ExitStack() as ctx:
+        keep = ctx.enter_context(tc.tile_pool(name="keep", bufs=1))
+        ring = ctx.enter_context(tc.tile_pool(name="ring", bufs=CHUNKS))
+        psum3 = ctx.enter_context(tc.psum_pool(name="psum3", bufs=3))
+        psum2 = ctx.enter_context(tc.psum_pool(name="psum2", bufs=2))
+
+        offsets = keep.tile([P, J // LANES], U16, name="offsets")
+        weight = keep.tile([P, J], F32, name="weight")
+        plane = [keep.tile([P, T], F32, name=f"plane{i}") for i in range(PACK)]
+        wg_raw = keep.tile([P, 2 * R], U8, name="wg_raw", align_bytes=64)
+        wu_raw = keep.tile([P, R], U32, name="wu_raw", align_bytes=64)
+        wd_raw = keep.tile([P, N], U32, name="wd_raw", align_bytes=64)
+        sc_raw = keep.tile([P, 3 * R], U8, name="sc_raw", align_bytes=64)
+        wg_c = keep.tile([P, 2 * R], U8, name="wg_c", align_bytes=64)
+        wu_c = keep.tile([P, R], U32, name="wu_c", align_bytes=64)
+        wd_c = keep.tile([P, N], U32, name="wd_c", align_bytes=64)
+        w_sc = keep.tile([P, 3 * R], U8, name="w_sc", align_bytes=64)
+        gate = [keep.tile([P, PACK, b - a], F32, name=f"gate{a}") for a, b in GATE_CUTS]
+        picked = keep.tile([P, 28 * C], F32, name="picked")
+        x_bf = keep.tile([P, PACK * J], BF16, name="x_bf", align_bytes=64)
+        h_bf = keep.tile([P, PACK * J], BF16, name="h_bf", align_bytes=64)
+        y_bf = keep.tile([P, PACK * J], BF16, name="y_bf", align_bytes=64)
+        x_codes = keep.tile([P, J], U32, name="x_codes", align_bytes=64)
+        h_codes = keep.tile([P, J], U32, name="h_codes", align_bytes=64)
+        y_codes = keep.tile([P, J], U32, name="y_codes", align_bytes=64)
+        x_sc = keep.tile([P, J], U8, name="x_sc", align_bytes=64)
+        h_sc = keep.tile([P, J], U8, name="h_sc", align_bytes=64)
+        y_sc = keep.tile([P, J], U8, name="y_sc", align_bytes=64)
+
+        x_rows = xT.rearrange("(p i) t -> p i t", i=PACK)
+        g_rows = g.rearrange("(p t) j -> p t j", t=PACK)
+        out_rows = out_0.rearrange("(p t) j -> p t j", t=PACK)
+        out_words = out_1[0].rearrange("p j i -> p (j i)").bitcast(I32)
+
+        def load_scales(a, scales):
+            for q in range(4):
+                rows = scales[0, 4 * q : 4 * q + 4, :].bitcast(I32)
+                nc.sync.dma_start(
+                    sc_raw[32 * q : 32 * (q + 1), a * R : (a + 1) * R].bitcast(I32),
+                    rows.unsqueeze(0).broadcast_to([8, 4, R // 4]),
+                )
+
+        def load_plane(n):
+            nc.sync.dma_start(plane[LOAD_ORDER[n]][:], x_rows[:, LOAD_ORDER[n], :])
+
+        nc.sync.dma_start(offsets[:], offs)
+        nc.sync.dma_start(weight[:, :FIRST], wgt[:, :FIRST])
+        load_plane(0)
+        load_scales(0, wg_scales)
+        nc.sync.dma_start(weight[:, FIRST:], wgt[:, FIRST:])
+        load_plane(1)
+        load_scales(1, wu_scales)
+        nc.sync.dma_start(wg_raw[:].bitcast(I32), wg_words[0].bitcast(I32))
+        nc.sync.dma_start(wu_raw[:].bitcast(I32), wu_words[0].rearrange("p r i -> p (r i)").bitcast(I32))
+        load_plane(2)
+        load_plane(3)
+        load_scales(2, wd_scales)
+        nc.sync.dma_start(wd_raw[:].bitcast(I32), wd_words[0].rearrange("p n i -> p (n i)").bitcast(I32))
+        for u, (a, b) in enumerate(GATE_CUTS):
+            nc.sync.dma_start(gate[u][:], g_rows[:, :, a:b])
+
+        def gather(i, j0, j1):
+            nc.vector.tensor_tensor(
+                picked[:, PLANE_AT[i] + j0 : PLANE_AT[i] + j1],
+                plane[i][:].indirect(offsets[:, j0 // LANES : j1 // LANES]),
+                weight[:, j0:j1],
+                MULT,
+            )
+
+        def deal(dst, src, width):
+            nc.vector.tensor_copy(
+                dst.rearrange("p (t m b) -> p m t b", t=PACK, b=width),
+                src.rearrange("p (m t b) -> p m t b", t=PACK, b=width),
+            )
+
+        def weave(dst, src):
+            nc.scalar.copy(
+                dst.rearrange("p (c i t) -> p c t i", i=4, t=PACK),
+                src.rearrange("p t (c i) -> p c t i", i=4),
+            )
+
+        def quantize(codes, scales, src, c):
+            nc.vector.quantize_mx(
+                out=codes[:, c * C : (c + 1) * C].bitcast(FP8X4),
+                scales=scales[:, c * C : (c + 1) * C],
+                in_=src[:, PACK * c * C : PACK * (c + 1) * C],
+            )
+
+        def product(acc, weights, a, codes, scales, c):
+            for t in range(PACK):
+                nc.tensor.matmul_mx(
+                    out=acc[:, t, :],
+                    lhsT=weights(t),
+                    lhsT_scale=w_sc[:, a * R + t * P : a * R + (t + 1) * P],
+                    rhs=codes[:, c * C : (c + 1) * C].bitcast(FP8X4),
+                    rhs_scale=scales[:, c * C : (c + 1) * C],
+                    start=True,
+                    stop=True,
+                )
+
+        def deal_scales(a):
+            deal(w_sc[:, a * R : (a + 1) * R], sc_raw[:, a * R : (a + 1) * R], 1)
+
+        gather(0, 0, FIRST)
+        gather(0, FIRST, J)
+        deal_scales(0)
+        gather(2, 0, FIRST)
+        gather(2, FIRST, J)
+        deal_scales(1)
+        deal(wg_c[:], wg_raw[:], 2)
+        deal(wu_c[:].bitcast(I32), wu_raw[:].bitcast(I32), 1)
+        gather(3, 0, FIRST)
+        gather(3, FIRST, J)
+
+        sig = {}
+        ub = {}
+        ysum = {}
+
+        def wide(c):
+            return slice(PACK * c * C, PACK * (c + 1) * C)
+
+        def stage_pick(c):
+            gather(1, c * C, (c + 1) * C)
+
+        def stage_round(c):
+            src = picked[:, c * C : (c + 20) * C].rearrange("p (u x j) -> p u x j", u=2, j=C)[:, :, 0:9:8, :]
+            nc.scalar.copy(
+                x_bf[:, wide(c)].rearrange("p (c i u e) -> p c u e i", i=4, u=2, e=2),
+                src.rearrange("p u e (c i) -> p c u e i", i=4),
+            )
+
+        def stage_up(c):
+            quantize(x_codes, x_sc, x_bf, c)
+            ga = psum3.tile([P, PACK, C], F32, name="ga")
+            ub[c] = psum3.tile([P, PACK, C], F32, name="ub")
+            product(ga, lambda t: wg_c[:, 2 * t * P : 2 * (t + 1) * P].bitcast(FP4X4), 0, x_codes, x_sc, c)
+            product(ub[c], lambda t: wu_c[:, t * P : (t + 1) * P].bitcast(FP8X4), 1, x_codes, x_sc, c)
+            sig[c] = ring.tile([P, C, PACK], F32, name="sig")
+            nc.scalar.activation(sig[c][:], ga[:].rearrange("p t j -> p j t"), SIGMOID)
+
+        def stage_glu(c):
+            nc.vector.tensor_tensor(
+                h_bf[:, wide(c)].rearrange("p (j t) -> p j t", t=PACK),
+                ub[c][:].rearrange("p t j -> p j t"),
+                sig[c][:],
+                MULT,
+            )
+
+        def stage_down(c):
+            quantize(h_codes, h_sc, h_bf, c)
+            ysum[c] = psum2.tile([P, PACK, C], F32, name="ysum")
+            product(ysum[c], lambda t: wd_c[:, t * P : (t + 1) * P].bitcast(FP8X4), 2, h_codes, h_sc, c)
+
+        def stage_gate(c):
+            u = [a <= c * C < b for a, b in GATE_CUTS].index(True)
+            j0 = c * C - GATE_CUTS[u][0]
+            res = ring.tile([P, PACK, C], F32, name="res")
+            nc.vector.tensor_tensor(
+                res[:], ysum[c][:], gate[u][:, :, j0 : j0 + C], MULT
+            )
+            weave(y_bf[:, wide(c)], res[:])
+            nc.sync.dma_start(out_rows[:, :, c * C : (c + 1) * C], res[:])
+
+        def stage_planes(c):
+            quantize(y_codes, y_sc, y_bf, c)
+            if c % 2 == 1:
+                cols = slice((c - 1) * C, (c + 1) * C)
+                nc.sync.dma_start(out_words[:, cols], y_codes[:, cols].bitcast(I32))
+
+        stages = (stage_pick, stage_round, stage_up, stage_glu, stage_down, stage_gate, stage_planes)
+        for step in range(CHUNKS + len(stages) - 1):
+            for depth in reversed(range(len(stages))):
+                c = step - depth
+                if 0 <= c < CHUNKS:
+                    stages[depth](c)
+            if step == 2:
+                deal_scales(2)
+                deal(wd_c[:].bitcast(I32), wd_raw[:].bitcast(I32), 1)
+
+        for q in range(4):
+            queue = nc.scalar if q % 2 else nc.sync
+            queue.dma_start(
+                out_2[0, 4 * q : 4 * q + 4, :].bitcast(I32), y_sc[32 * q : 32 * q + 4, :].bitcast(I32)
+            )

@@ -22,8 +22,14 @@ C = 128
 CHUNKS = J // C
 LANES = 16
 FIRST = 256
-PLANE_AT = (0, 8 * C, 10 * C, 18 * C)
-LOAD_ORDER = (0, 2, 3, 1)
+HOLD = 4
+PICK_GROUPS = ((0,), (1,), (2, 3), (4, 5), (6, 7))
+PLANE_AT = (0, J, 2 * J, 2 * J + HOLD * C)
+EARLY_CUTS = ((0, 256), (256, 640), (640, 1024))
+PLANE_GROUPS = ((0, 1, 2, 3), (4, 5), (6,), (7,))
+WORD_STORES = ((0, 6), (6, 8))
+LAG = (0, 4, 10, 18, 25, 34, 43, 50)
+LOAD_ORDER = (0, 1, 3, 2)
 GATE_CUTS = ((0, 256), (256, 512), (512, 1024))
 
 
@@ -43,13 +49,15 @@ def tile_list_sigm_mulP_kernel(
         wg_raw = keep.tile([P, 2 * R], U8, name="wg_raw", align_bytes=64)
         wu_raw = keep.tile([P, R], U32, name="wu_raw", align_bytes=64)
         wd_raw = keep.tile([P, N], U32, name="wd_raw", align_bytes=64)
-        sc_raw = keep.tile([P, 3 * R], U8, name="sc_raw", align_bytes=64)
+        g_sc_raw = keep.tile([P, R], U8, name="g_sc_raw", align_bytes=64)
+        ud_sc_raw = keep.tile([P, R], U8, name="ud_sc_raw", align_bytes=64)
         wg_c = keep.tile([P, 2 * R], U8, name="wg_c", align_bytes=64)
         wu_c = keep.tile([P, R], U32, name="wu_c", align_bytes=64)
         wd_c = keep.tile([P, N], U32, name="wd_c", align_bytes=64)
-        w_sc = keep.tile([P, 3 * R], U8, name="w_sc", align_bytes=64)
+        g_sc = keep.tile([P, R], U8, name="g_sc", align_bytes=64)
+        ud_sc = keep.tile([P, R], U8, name="ud_sc", align_bytes=64)
         gate = [keep.tile([P, PACK, b - a], F32, name=f"gate{a}") for a, b in GATE_CUTS]
-        picked = keep.tile([P, 28 * C], F32, name="picked")
+        picked = keep.tile([P, 3 * J + 2 * HOLD * C], F32, name="picked")
         x_bf = keep.tile([P, PACK * J], BF16, name="x_bf", align_bytes=64)
         h_bf = keep.tile([P, PACK * J], BF16, name="h_bf", align_bytes=64)
         y_bf = keep.tile([P, PACK * J], BF16, name="y_bf", align_bytes=64)
@@ -65,29 +73,35 @@ def tile_list_sigm_mulP_kernel(
         out_rows = out_0.rearrange("(p t) j -> p t j", t=PACK)
         out_words = out_1[0].rearrange("p j i -> p (j i)").bitcast(I32)
 
-        def load_scales(a, scales):
-            for q in range(4):
-                rows = scales[0, 4 * q : 4 * q + 4, :].bitcast(I32)
-                nc.sync.dma_start(
-                    sc_raw[32 * q : 32 * (q + 1), a * R : (a + 1) * R].bitcast(I32),
-                    rows.unsqueeze(0).broadcast_to([8, 4, R // 4]),
-                )
-
         def load_plane(n):
             nc.sync.dma_start(plane[LOAD_ORDER[n]][:], x_rows[:, LOAD_ORDER[n], :])
 
+        def load_packed_scales(first, last):
+            for n in range(first, last):
+                a, q = divmod(n, 4)
+                nc.sync.dma_start(
+                    ud_sc_raw[32 * q + 4 * a : 32 * q + 4 * a + 4, :].bitcast(I32),
+                    (wu_scales, wd_scales)[a][0, 4 * q : 4 * q + 4, :].bitcast(I32),
+                )
+
+        nc.gpsimd.memset(ud_sc_raw[:].bitcast(I32), 0)
         nc.sync.dma_start(offsets[:], offs)
         nc.sync.dma_start(weight[:, :FIRST], wgt[:, :FIRST])
+        nc.sync.dma_start(wg_raw[:].bitcast(I32), wg_words[0].bitcast(I32))
+        for q in range(4):
+            rows = wg_scales[0, 4 * q : 4 * q + 4, :].bitcast(I32)
+            nc.sync.dma_start(
+                g_sc_raw[32 * q : 32 * (q + 1), :].bitcast(I32),
+                rows.unsqueeze(0).broadcast_to([8, 4, R // 4]),
+            )
         load_plane(0)
-        load_scales(0, wg_scales)
         nc.sync.dma_start(weight[:, FIRST:], wgt[:, FIRST:])
         load_plane(1)
-        load_scales(1, wu_scales)
-        nc.sync.dma_start(wg_raw[:].bitcast(I32), wg_words[0].bitcast(I32))
-        nc.sync.dma_start(wu_raw[:].bitcast(I32), wu_words[0].rearrange("p r i -> p (r i)").bitcast(I32))
+        load_packed_scales(0, 5)
         load_plane(2)
         load_plane(3)
-        load_scales(2, wd_scales)
+        load_packed_scales(5, 8)
+        nc.sync.dma_start(wu_raw[:].bitcast(I32), wu_words[0].rearrange("p r i -> p (r i)").bitcast(I32))
         nc.sync.dma_start(wd_raw[:].bitcast(I32), wd_words[0].rearrange("p n i -> p (n i)").bitcast(I32))
         for u, (a, b) in enumerate(GATE_CUTS):
             nc.sync.dma_start(gate[u][:], g_rows[:, :, a:b])
@@ -100,74 +114,80 @@ def tile_list_sigm_mulP_kernel(
                 MULT,
             )
 
-        def deal(dst, src, width):
+        def deal_bytes(dst, src, width):
             nc.vector.tensor_copy(
-                dst.rearrange("p (t m b) -> p m t b", t=PACK, b=width),
-                src.rearrange("p (m t b) -> p m t b", t=PACK, b=width),
+                dst.rearrange("p (t m b) -> p t m b", t=PACK, b=width),
+                src.rearrange("p (m t b) -> p t m b", t=PACK, b=width),
             )
 
-        def weave(dst, src):
-            nc.scalar.copy(
-                dst.rearrange("p (c i t) -> p c t i", i=4, t=PACK),
-                src.rearrange("p t (c i) -> p c t i", i=4),
+        def deal_words(dst, src):
+            nc.vector.tensor_copy(
+                dst[:].bitcast(I32).rearrange("p (t m i) -> p m t i", t=PACK, i=4),
+                src[:].bitcast(I32).rearrange("p (m i t) -> p m t i", t=PACK, i=4),
             )
 
-        def quantize(codes, scales, src, c):
+        def weave(dst, src, copy):
+            copy(
+                dst.rearrange("p (c i t) -> p c t i", i=2, t=PACK),
+                src.rearrange("p t (c i) -> p c t i", i=2),
+            )
+
+        def quantize(codes, scales, src, c0, c1):
             nc.vector.quantize_mx(
-                out=codes[:, c * C : (c + 1) * C].bitcast(FP8X4),
-                scales=scales[:, c * C : (c + 1) * C],
-                in_=src[:, PACK * c * C : PACK * (c + 1) * C],
+                out=codes[:, c0 * C : c1 * C].bitcast(FP8X4),
+                scales=scales[:, c0 * C : c1 * C],
+                in_=src[:, PACK * c0 * C : PACK * c1 * C],
             )
 
-        def product(acc, weights, a, codes, scales, c):
+        def product(acc, weights, w_sc, codes, scales, c):
             for t in range(PACK):
                 nc.tensor.matmul_mx(
                     out=acc[:, t, :],
                     lhsT=weights(t),
-                    lhsT_scale=w_sc[:, a * R + t * P : a * R + (t + 1) * P],
+                    lhsT_scale=w_sc[:, t * P : (t + 1) * P],
                     rhs=codes[:, c * C : (c + 1) * C].bitcast(FP8X4),
                     rhs_scale=scales[:, c * C : (c + 1) * C],
                     start=True,
                     stop=True,
                 )
 
-        def deal_scales(a):
-            deal(w_sc[:, a * R : (a + 1) * R], sc_raw[:, a * R : (a + 1) * R], 1)
-
-        gather(0, 0, FIRST)
-        gather(0, FIRST, J)
-        deal_scales(0)
-        gather(2, 0, FIRST)
-        gather(2, FIRST, J)
-        deal_scales(1)
-        deal(wg_c[:], wg_raw[:], 2)
-        deal(wu_c[:].bitcast(I32), wu_raw[:].bitcast(I32), 1)
-        gather(3, 0, FIRST)
-        gather(3, FIRST, J)
+        x_quads = x_bf[:].rearrange("p (j t) -> p j t", t=PACK)
+        deal_bytes(wg_c[:], wg_raw[:], 2)
+        deal_bytes(g_sc[:], g_sc_raw[:], 1)
+        for n in range(3):
+            gather(LOAD_ORDER[n], 0, FIRST)
+            gather(LOAD_ORDER[n], FIRST, J)
+            if n == 1:
+                early = picked[:, : 2 * J].rearrange("p (e j) -> p j e", e=2)
+                for a, b in EARLY_CUTS:
+                    nc.scalar.copy(x_quads[:, a:b, 0:2], early[:, a:b, :])
 
         sig = {}
         ub = {}
         ysum = {}
+        res = {}
 
         def wide(c):
             return slice(PACK * c * C, PACK * (c + 1) * C)
 
         def stage_pick(c):
-            gather(1, c * C, (c + 1) * C)
+            for group in PICK_GROUPS:
+                if c == group[0]:
+                    gather(LOAD_ORDER[3], c * C, (group[-1] + 1) * C)
 
         def stage_round(c):
-            src = picked[:, c * C : (c + 20) * C].rearrange("p (u x j) -> p u x j", u=2, j=C)[:, :, 0:9:8, :]
+            late = picked[:, PLANE_AT[2] + c * C : PLANE_AT[2] + (c + 2 * HOLD) * C]
             nc.scalar.copy(
-                x_bf[:, wide(c)].rearrange("p (c i u e) -> p c u e i", i=4, u=2, e=2),
-                src.rearrange("p u e (c i) -> p c u e i", i=4),
+                x_quads[:, c * C : (c + 1) * C, 2:4],
+                late.rearrange("p (e x) -> p x e", e=2)[:, :C, :],
             )
 
         def stage_up(c):
-            quantize(x_codes, x_sc, x_bf, c)
+            quantize(x_codes, x_sc, x_bf, c, c + 1)
             ga = psum3.tile([P, PACK, C], F32, name="ga")
-            ub[c] = psum3.tile([P, PACK, C], F32, name="ub")
-            product(ga, lambda t: wg_c[:, 2 * t * P : 2 * (t + 1) * P].bitcast(FP4X4), 0, x_codes, x_sc, c)
-            product(ub[c], lambda t: wu_c[:, t * P : (t + 1) * P].bitcast(FP8X4), 1, x_codes, x_sc, c)
+            ub[c] = psum2.tile([P, PACK, C], F32, name="ub")
+            product(ga, lambda t: wg_c[:, 2 * t * P : 2 * (t + 1) * P].bitcast(FP4X4), g_sc[:], x_codes, x_sc, c)
+            product(ub[c], lambda t: wu_c[:, t * P : (t + 1) * P].bitcast(FP8X4), ud_sc[:], x_codes, x_sc, c)
             sig[c] = ring.tile([P, C, PACK], F32, name="sig")
             nc.scalar.activation(sig[c][:], ga[:].rearrange("p t j -> p j t"), SIGMOID)
 
@@ -180,35 +200,36 @@ def tile_list_sigm_mulP_kernel(
             )
 
         def stage_down(c):
-            quantize(h_codes, h_sc, h_bf, c)
-            ysum[c] = psum2.tile([P, PACK, C], F32, name="ysum")
-            product(ysum[c], lambda t: wd_c[:, t * P : (t + 1) * P].bitcast(FP8X4), 2, h_codes, h_sc, c)
+            quantize(h_codes, h_sc, h_bf, c, c + 1)
+            ysum[c] = psum3.tile([P, PACK, C], F32, name="ysum")
+            product(ysum[c], lambda t: wd_c[:, t * P : (t + 1) * P].bitcast(FP8X4), ud_sc[4:, :], h_codes, h_sc, c)
 
         def stage_gate(c):
             u = [a <= c * C < b for a, b in GATE_CUTS].index(True)
             j0 = c * C - GATE_CUTS[u][0]
-            res = ring.tile([P, PACK, C], F32, name="res")
-            nc.vector.tensor_tensor(
-                res[:], ysum[c][:], gate[u][:, :, j0 : j0 + C], MULT
-            )
-            weave(y_bf[:, wide(c)], res[:])
-            nc.sync.dma_start(out_rows[:, :, c * C : (c + 1) * C], res[:])
+            res[c] = ring.tile([P, PACK, C], F32, name="res")
+            nc.vector.tensor_tensor(res[c][:], ysum[c][:], gate[u][:, :, j0 : j0 + C], MULT)
+            nc.sync.dma_start(out_rows[:, :, c * C : (c + 1) * C], res[c][:])
+
+        def stage_yround(c):
+            weave(y_bf[:, wide(c)], res[c][:], nc.vector.tensor_copy if c == CHUNKS - 1 else nc.scalar.copy)
 
         def stage_planes(c):
-            quantize(y_codes, y_sc, y_bf, c)
-            if c % 2 == 1:
-                cols = slice((c - 1) * C, (c + 1) * C)
-                nc.sync.dma_start(out_words[:, cols], y_codes[:, cols].bitcast(I32))
+            for group in PLANE_GROUPS:
+                if c == group[-1]:
+                    quantize(y_codes, y_sc, y_bf, group[0], c + 1)
+            for c0, c1 in WORD_STORES:
+                if c == c1 - 1:
+                    nc.sync.dma_start(out_words[:, c0 * C : c1 * C], y_codes[:, c0 * C : c1 * C].bitcast(I32))
 
-        stages = (stage_pick, stage_round, stage_up, stage_glu, stage_down, stage_gate, stage_planes)
-        for step in range(CHUNKS + len(stages) - 1):
-            for depth in reversed(range(len(stages))):
-                c = step - depth
-                if 0 <= c < CHUNKS:
-                    stages[depth](c)
-            if step == 2:
-                deal_scales(2)
-                deal(wd_c[:].bitcast(I32), wd_raw[:].bitcast(I32), 1)
+        stages = (stage_pick, stage_round, stage_up, stage_glu, stage_down, stage_gate, stage_yround, stage_planes)
+        for place, depth, c in sorted((4 * c + LAG[d], d, c) for d in range(len(stages)) for c in range(CHUNKS)):
+            stages[depth](c)
+            if depth == 0 and c == 1:
+                deal_bytes(ud_sc[:], ud_sc_raw[:], 1)
+                deal_words(wu_c, wu_raw)
+            if depth == 2 and c == 1:
+                deal_words(wd_c, wd_raw)
 
         for q in range(4):
             queue = nc.scalar if q % 2 else nc.sync

@@ -25,7 +25,8 @@ FIRST = 256
 HOLD = 4
 PICK_GROUPS = ((0,), (1,), (2, 3), (4, 5), (6, 7))
 PLANE_AT = (0, J, 2 * J, 2 * J + HOLD * C)
-EARLY_CUTS = ((0, 256), (256, 640), (640, 1024))
+EARLY_PICKS = (((0, FIRST), (FIRST, J)), ((0, 512), (512, J)), ((0, J),))
+EARLY_CUTS = ((0, 512), (512, 1024))
 PLANE_GROUPS = ((0, 1, 2, 3), (4, 5), (6,), (7,))
 WORD_STORES = ((0, 6), (6, 8))
 LAG = (0, 4, 10, 18, 25, 34, 43, 50)
@@ -49,13 +50,11 @@ def tile_list_sigm_mulP_kernel(
         wg_raw = keep.tile([P, 2 * R], U8, name="wg_raw", align_bytes=64)
         wu_raw = keep.tile([P, R], U32, name="wu_raw", align_bytes=64)
         wd_raw = keep.tile([P, N], U32, name="wd_raw", align_bytes=64)
-        g_sc_raw = keep.tile([P, R], U8, name="g_sc_raw", align_bytes=64)
-        ud_sc_raw = keep.tile([P, R], U8, name="ud_sc_raw", align_bytes=64)
+        w_sc_raw = keep.tile([P, R], U8, name="w_sc_raw", align_bytes=64)
         wg_c = keep.tile([P, 2 * R], U8, name="wg_c", align_bytes=64)
         wu_c = keep.tile([P, R], U32, name="wu_c", align_bytes=64)
         wd_c = keep.tile([P, N], U32, name="wd_c", align_bytes=64)
-        g_sc = keep.tile([P, R], U8, name="g_sc", align_bytes=64)
-        ud_sc = keep.tile([P, R], U8, name="ud_sc", align_bytes=64)
+        w_sc = keep.tile([P, R], U8, name="w_sc", align_bytes=64)
         gate = [keep.tile([P, PACK, b - a], F32, name=f"gate{a}") for a, b in GATE_CUTS]
         picked = keep.tile([P, 3 * J + 2 * HOLD * C], F32, name="picked")
         x_bf = keep.tile([P, PACK * J], BF16, name="x_bf", align_bytes=64)
@@ -76,32 +75,27 @@ def tile_list_sigm_mulP_kernel(
         def load_plane(n):
             nc.sync.dma_start(plane[LOAD_ORDER[n]][:], x_rows[:, LOAD_ORDER[n], :])
 
-        def load_packed_scales(first, last):
+        def load_scales(first, last):
             for n in range(first, last):
                 a, q = divmod(n, 4)
                 nc.sync.dma_start(
-                    ud_sc_raw[32 * q + 4 * a : 32 * q + 4 * a + 4, :].bitcast(I32),
-                    (wu_scales, wd_scales)[a][0, 4 * q : 4 * q + 4, :].bitcast(I32),
+                    w_sc_raw[32 * q + 4 * a : 32 * q + 4 * a + 4, :].bitcast(I32),
+                    (wg_scales, wu_scales, wd_scales)[a][0, 4 * q : 4 * q + 4, :].bitcast(I32),
                 )
 
-        nc.gpsimd.memset(ud_sc_raw[:].bitcast(I32), 0)
+        nc.vector.memset(w_sc_raw[:].bitcast(I32), 0)
         nc.sync.dma_start(offsets[:], offs)
         nc.sync.dma_start(weight[:, :FIRST], wgt[:, :FIRST])
-        nc.sync.dma_start(wg_raw[:].bitcast(I32), wg_words[0].bitcast(I32))
-        for q in range(4):
-            rows = wg_scales[0, 4 * q : 4 * q + 4, :].bitcast(I32)
-            nc.sync.dma_start(
-                g_sc_raw[32 * q : 32 * (q + 1), :].bitcast(I32),
-                rows.unsqueeze(0).broadcast_to([8, 4, R // 4]),
-            )
         load_plane(0)
         nc.sync.dma_start(weight[:, FIRST:], wgt[:, FIRST:])
+        nc.sync.dma_start(wg_raw[:].bitcast(I32), wg_words[0].bitcast(I32))
+        load_scales(0, 3)
         load_plane(1)
-        load_packed_scales(0, 5)
-        load_plane(2)
-        load_plane(3)
-        load_packed_scales(5, 8)
+        load_scales(3, 7)
         nc.sync.dma_start(wu_raw[:].bitcast(I32), wu_words[0].rearrange("p r i -> p (r i)").bitcast(I32))
+        load_plane(2)
+        load_scales(7, 12)
+        load_plane(3)
         nc.sync.dma_start(wd_raw[:].bitcast(I32), wd_words[0].rearrange("p n i -> p (n i)").bitcast(I32))
         for u, (a, b) in enumerate(GATE_CUTS):
             nc.sync.dma_start(gate[u][:], g_rows[:, :, a:b])
@@ -139,12 +133,12 @@ def tile_list_sigm_mulP_kernel(
                 in_=src[:, PACK * c0 * C : PACK * c1 * C],
             )
 
-        def product(acc, weights, w_sc, codes, scales, c):
+        def product(acc, weights, rows, codes, scales, c):
             for t in range(PACK):
                 nc.tensor.matmul_mx(
                     out=acc[:, t, :],
                     lhsT=weights(t),
-                    lhsT_scale=w_sc[:, t * P : (t + 1) * P],
+                    lhsT_scale=rows[:, t * P : (t + 1) * P],
                     rhs=codes[:, c * C : (c + 1) * C].bitcast(FP8X4),
                     rhs_scale=scales[:, c * C : (c + 1) * C],
                     start=True,
@@ -152,11 +146,15 @@ def tile_list_sigm_mulP_kernel(
                 )
 
         x_quads = x_bf[:].rearrange("p (j t) -> p j t", t=PACK)
-        deal_bytes(wg_c[:], wg_raw[:], 2)
-        deal_bytes(g_sc[:], g_sc_raw[:], 1)
         for n in range(3):
-            gather(LOAD_ORDER[n], 0, FIRST)
-            gather(LOAD_ORDER[n], FIRST, J)
+            for a, b in EARLY_PICKS[n]:
+                gather(LOAD_ORDER[n], a, b)
+            if n == 0:
+                deal_bytes(wg_c[:], wg_raw[:], 2)
+            if n == 1:
+                deal_words(wu_c, wu_raw)
+            if n == 2:
+                deal_bytes(w_sc[:], w_sc_raw[:], 1)
             if n == 1:
                 early = picked[:, : 2 * J].rearrange("p (e j) -> p j e", e=2)
                 for a, b in EARLY_CUTS:
@@ -186,8 +184,8 @@ def tile_list_sigm_mulP_kernel(
             quantize(x_codes, x_sc, x_bf, c, c + 1)
             ga = psum3.tile([P, PACK, C], F32, name="ga")
             ub[c] = psum2.tile([P, PACK, C], F32, name="ub")
-            product(ga, lambda t: wg_c[:, 2 * t * P : 2 * (t + 1) * P].bitcast(FP4X4), g_sc[:], x_codes, x_sc, c)
-            product(ub[c], lambda t: wu_c[:, t * P : (t + 1) * P].bitcast(FP8X4), ud_sc[:], x_codes, x_sc, c)
+            product(ga, lambda t: wg_c[:, 2 * t * P : 2 * (t + 1) * P].bitcast(FP4X4), w_sc[:], x_codes, x_sc, c)
+            product(ub[c], lambda t: wu_c[:, t * P : (t + 1) * P].bitcast(FP8X4), w_sc[4:, :], x_codes, x_sc, c)
             sig[c] = ring.tile([P, C, PACK], F32, name="sig")
             nc.scalar.activation(sig[c][:], ga[:].rearrange("p t j -> p j t"), SIGMOID)
 
@@ -202,7 +200,7 @@ def tile_list_sigm_mulP_kernel(
         def stage_down(c):
             quantize(h_codes, h_sc, h_bf, c, c + 1)
             ysum[c] = psum3.tile([P, PACK, C], F32, name="ysum")
-            product(ysum[c], lambda t: wd_c[:, t * P : (t + 1) * P].bitcast(FP8X4), ud_sc[4:, :], h_codes, h_sc, c)
+            product(ysum[c], lambda t: wd_c[:, t * P : (t + 1) * P].bitcast(FP8X4), w_sc[8:, :], h_codes, h_sc, c)
 
         def stage_gate(c):
             u = [a <= c * C < b for a, b in GATE_CUTS].index(True)
@@ -225,9 +223,6 @@ def tile_list_sigm_mulP_kernel(
         stages = (stage_pick, stage_round, stage_up, stage_glu, stage_down, stage_gate, stage_yround, stage_planes)
         for place, depth, c in sorted((4 * c + LAG[d], d, c) for d in range(len(stages)) for c in range(CHUNKS)):
             stages[depth](c)
-            if depth == 0 and c == 1:
-                deal_bytes(ud_sc[:], ud_sc_raw[:], 1)
-                deal_words(wu_c, wu_raw)
             if depth == 2 and c == 1:
                 deal_words(wd_c, wd_raw)
 

@@ -22,16 +22,14 @@ C = 128
 CHUNKS = J // C
 LANES = 16
 FIRST = 256
-HOLD = 4
-PICK_GROUPS = ((0,), (1,), (2, 3), (4, 5), (6, 7))
+HOLD = 3
 PLANE_AT = (0, J, 2 * J, 2 * J + HOLD * C)
 EARLY_PICKS = (((0, FIRST), (FIRST, J)), ((0, 512), (512, J)), ((0, J),))
 EARLY_CUTS = ((0, 512), (512, 1024))
-PLANE_GROUPS = ((0, 1, 2, 3), (4, 5), (6,), (7,))
-WORD_STORES = ((0, 6), (6, 8))
-LAG = (0, 4, 10, 18, 25, 34, 43, 50)
+PLANE_GROUPS = ((0, 4), (4, 6), (6, 8))
+LAG = (0, 1, 2, 4, 5, 7, 9)
 LOAD_ORDER = (0, 1, 3, 2)
-GATE_CUTS = ((0, 256), (256, 512), (512, 1024))
+GATE_CUTS = ((0, 512), (512, 1024))
 
 
 def tile_list_sigm_mulP_kernel(
@@ -133,17 +131,16 @@ def tile_list_sigm_mulP_kernel(
                 in_=src[:, PACK * c0 * C : PACK * c1 * C],
             )
 
-        def product(acc, weights, rows, codes, scales, c):
-            for t in range(PACK):
-                nc.tensor.matmul_mx(
-                    out=acc[:, t, :],
-                    lhsT=weights(t),
-                    lhsT_scale=rows[:, t * P : (t + 1) * P],
-                    rhs=codes[:, c * C : (c + 1) * C].bitcast(FP8X4),
-                    rhs_scale=scales[:, c * C : (c + 1) * C],
-                    start=True,
-                    stop=True,
-                )
+        def product(acc, weights, first_row, t, codes, scales, cols):
+            nc.tensor.matmul_mx(
+                out=acc,
+                lhsT=weights,
+                lhsT_scale=w_sc[first_row:, t * P : (t + 1) * P],
+                rhs=codes[:, cols].bitcast(FP8X4),
+                rhs_scale=scales[:, cols],
+                start=True,
+                stop=True,
+            )
 
         x_quads = x_bf[:].rearrange("p (j t) -> p j t", t=PACK)
         for n in range(3):
@@ -169,9 +166,7 @@ def tile_list_sigm_mulP_kernel(
             return slice(PACK * c * C, PACK * (c + 1) * C)
 
         def stage_pick(c):
-            for group in PICK_GROUPS:
-                if c == group[0]:
-                    gather(LOAD_ORDER[3], c * C, (group[-1] + 1) * C)
+            gather(LOAD_ORDER[3], c * C, (c + 1) * C)
 
         def stage_round(c):
             late = picked[:, PLANE_AT[2] + c * C : PLANE_AT[2] + (c + 2 * HOLD) * C]
@@ -182,12 +177,17 @@ def tile_list_sigm_mulP_kernel(
 
         def stage_up(c):
             quantize(x_codes, x_sc, x_bf, c, c + 1)
-            ga = psum3.tile([P, PACK, C], F32, name="ga")
-            ub[c] = psum2.tile([P, PACK, C], F32, name="ub")
-            product(ga, lambda t: wg_c[:, 2 * t * P : 2 * (t + 1) * P].bitcast(FP4X4), w_sc[:], x_codes, x_sc, c)
-            product(ub[c], lambda t: wu_c[:, t * P : (t + 1) * P].bitcast(FP8X4), w_sc[4:, :], x_codes, x_sc, c)
+            ga = psum2.tile([P, PACK, C], F32, name="ga")
+            ub[c] = psum3.tile([P, PACK, C], F32, name="ub")
+            cols = slice(c * C, (c + 1) * C)
+            for t in range(PACK):
+                product(ga[:, t, :], wg_c[:, 2 * t * P : 2 * (t + 1) * P].bitcast(FP4X4), 0, t, x_codes, x_sc, cols)
+            for t in range(PACK):
+                product(ub[c][:, t, :], wu_c[:, t * P : (t + 1) * P].bitcast(FP8X4), 4, t, x_codes, x_sc, cols)
             sig[c] = ring.tile([P, C, PACK], F32, name="sig")
             nc.scalar.activation(sig[c][:], ga[:].rearrange("p t j -> p j t"), SIGMOID)
+            if c == 1:
+                deal_words(wd_c, wd_raw)
 
         def stage_glu(c):
             nc.vector.tensor_tensor(
@@ -199,32 +199,37 @@ def tile_list_sigm_mulP_kernel(
 
         def stage_down(c):
             quantize(h_codes, h_sc, h_bf, c, c + 1)
-            ysum[c] = psum3.tile([P, PACK, C], F32, name="ysum")
-            product(ysum[c], lambda t: wd_c[:, t * P : (t + 1) * P].bitcast(FP8X4), w_sc[8:, :], h_codes, h_sc, c)
+            if c % 2 == 1:
+                cols = slice((c - 1) * C, (c + 1) * C)
+                for u in range(2):
+                    ysum[c - 1 + u] = psum3.tile([P, 2, 2 * C], F32, name="ysum")
+                    for t in (2 * u, 2 * u + 1):
+                        weights = wd_c[:, t * P : (t + 1) * P].bitcast(FP8X4)
+                        product(ysum[c - 1 + u][:, t % 2, :], weights, 8, t, h_codes, h_sc, cols)
 
         def stage_gate(c):
-            u = [a <= c * C < b for a, b in GATE_CUTS].index(True)
-            j0 = c * C - GATE_CUTS[u][0]
-            res[c] = ring.tile([P, PACK, C], F32, name="res")
-            nc.vector.tensor_tensor(res[c][:], ysum[c][:], gate[u][:, :, j0 : j0 + C], MULT)
-            nc.sync.dma_start(out_rows[:, :, c * C : (c + 1) * C], res[c][:])
+            n, u = divmod(c, 2)
+            rows = slice(2 * u, 2 * u + 2)
+            if u == 0:
+                res[n] = keep.tile([P, PACK, 2 * C], F32, name=f"res{n}")
+            half, j0 = divmod(2 * n * C, J // 2)
+            nc.vector.tensor_tensor(res[n][:, rows, :], ysum[c][:], gate[half][:, rows, j0 : j0 + 2 * C], MULT)
+            nc.sync.dma_start(out_rows[:, rows, 2 * n * C : 2 * (n + 1) * C], res[n][:, rows, :])
 
         def stage_yround(c):
-            weave(y_bf[:, wide(c)], res[c][:], nc.vector.tensor_copy if c == CHUNKS - 1 else nc.scalar.copy)
-
-        def stage_planes(c):
-            for group in PLANE_GROUPS:
-                if c == group[-1]:
-                    quantize(y_codes, y_sc, y_bf, group[0], c + 1)
-            for c0, c1 in WORD_STORES:
+            n, u = divmod(c, 2)
+            copy = nc.vector.tensor_copy if c == CHUNKS - 1 else nc.scalar.copy
+            weave(y_bf[:, wide(c)], res[n][:, :, u * C : (u + 1) * C], copy)
+            for c0, c1 in PLANE_GROUPS:
                 if c == c1 - 1:
+                    quantize(y_codes, y_sc, y_bf, c0, c1)
                     nc.sync.dma_start(out_words[:, c0 * C : c1 * C], y_codes[:, c0 * C : c1 * C].bitcast(I32))
 
-        stages = (stage_pick, stage_round, stage_up, stage_glu, stage_down, stage_gate, stage_yround, stage_planes)
-        for place, depth, c in sorted((4 * c + LAG[d], d, c) for d in range(len(stages)) for c in range(CHUNKS)):
-            stages[depth](c)
-            if depth == 2 and c == 1:
-                deal_words(wd_c, wd_raw)
+        stages = (stage_pick, stage_round, stage_up, stage_glu, stage_down, stage_gate, stage_yround)
+        for step in range(CHUNKS + LAG[-1]):
+            for stage, lag in zip(stages, LAG):
+                if 0 <= step - lag < CHUNKS:
+                    stage(step - lag)
 
         for q in range(4):
             queue = nc.scalar if q % 2 else nc.sync

@@ -23,11 +23,14 @@ CHUNKS = J // C
 LANES = 16
 FIRST = 256
 HOLD = 3
+LAST_CUT = 80
+PAIRS = CHUNKS // 2
+SIDE = 2
 PLANE_AT = (0, J, 2 * J, 2 * J + HOLD * C)
 EARLY_PICKS = (((0, FIRST), (FIRST, J)), ((0, 512), (512, J)), ((0, J),))
 EARLY_CUTS = ((0, 512), (512, 1024))
 PLANE_GROUPS = ((0, 4), (4, 6), (6, 8))
-LAG = (0, 1, 2, 4, 5, 7, 9)
+LAG = (0, 1, 2, 4, 5, 8, 10)
 LOAD_ORDER = (0, 1, 3, 2)
 GATE_CUTS = ((0, 512), (512, 1024))
 
@@ -56,7 +59,9 @@ def tile_list_sigm_mulP_kernel(
         gate = [keep.tile([P, PACK, b - a], F32, name=f"gate{a}") for a, b in GATE_CUTS]
         picked = keep.tile([P, 3 * J + 2 * HOLD * C], F32, name="picked")
         x_bf = keep.tile([P, PACK * J], BF16, name="x_bf", align_bytes=64)
-        h_bf = keep.tile([P, PACK * J], BF16, name="h_bf", align_bytes=64)
+        res = [keep.tile([P, 2 * PACK * C], F32, name=f"res{n}", align_bytes=64) for n in range(PAIRS)]
+        h_own = [keep.tile([P, 2 * PACK * C], BF16, name=f"h_own{n}", align_bytes=64) for n in range(PAIRS - SIDE)]
+        h_bf = [h_own[0][:]] + [res[n][:, : PACK * C].bitcast(BF16) for n in range(SIDE)] + [h[:] for h in h_own[1:]]
         y_bf = keep.tile([P, PACK * J], BF16, name="y_bf", align_bytes=64)
         x_codes = keep.tile([P, J], U32, name="x_codes", align_bytes=64)
         h_codes = keep.tile([P, J], U32, name="h_codes", align_bytes=64)
@@ -84,16 +89,16 @@ def tile_list_sigm_mulP_kernel(
         nc.vector.memset(w_sc_raw[:].bitcast(I32), 0)
         nc.sync.dma_start(offsets[:], offs)
         nc.sync.dma_start(weight[:, :FIRST], wgt[:, :FIRST])
+        nc.sync.dma_start(wg_raw[:].bitcast(I32), wg_words[0].bitcast(I32))
         load_plane(0)
         nc.sync.dma_start(weight[:, FIRST:], wgt[:, FIRST:])
-        nc.sync.dma_start(wg_raw[:].bitcast(I32), wg_words[0].bitcast(I32))
         load_scales(0, 3)
         load_plane(1)
-        load_scales(3, 7)
-        nc.sync.dma_start(wu_raw[:].bitcast(I32), wu_words[0].rearrange("p r i -> p (r i)").bitcast(I32))
+        load_scales(3, 8)
         load_plane(2)
-        load_scales(7, 12)
+        load_scales(8, 12)
         load_plane(3)
+        nc.sync.dma_start(wu_raw[:].bitcast(I32), wu_words[0].rearrange("p r i -> p (r i)").bitcast(I32))
         nc.sync.dma_start(wd_raw[:].bitcast(I32), wd_words[0].rearrange("p n i -> p (n i)").bitcast(I32))
         for u, (a, b) in enumerate(GATE_CUTS):
             nc.sync.dma_start(gate[u][:], g_rows[:, :, a:b])
@@ -128,7 +133,7 @@ def tile_list_sigm_mulP_kernel(
             nc.vector.quantize_mx(
                 out=codes[:, c0 * C : c1 * C].bitcast(FP8X4),
                 scales=scales[:, c0 * C : c1 * C],
-                in_=src[:, PACK * c0 * C : PACK * c1 * C],
+                in_=src,
             )
 
         def product(acc, weights, first_row, t, codes, scales, cols):
@@ -143,13 +148,10 @@ def tile_list_sigm_mulP_kernel(
             )
 
         x_quads = x_bf[:].rearrange("p (j t) -> p j t", t=PACK)
+        deal_bytes(wg_c[:], wg_raw[:], 2)
         for n in range(3):
             for a, b in EARLY_PICKS[n]:
                 gather(LOAD_ORDER[n], a, b)
-            if n == 0:
-                deal_bytes(wg_c[:], wg_raw[:], 2)
-            if n == 1:
-                deal_words(wu_c, wu_raw)
             if n == 2:
                 deal_bytes(w_sc[:], w_sc_raw[:], 1)
             if n == 1:
@@ -160,13 +162,15 @@ def tile_list_sigm_mulP_kernel(
         sig = {}
         ub = {}
         ysum = {}
-        res = {}
+        y_sb = {}
 
         def wide(c):
             return slice(PACK * c * C, PACK * (c + 1) * C)
 
         def stage_pick(c):
             gather(LOAD_ORDER[3], c * C, (c + 1) * C)
+            if c == 1:
+                deal_words(wu_c, wu_raw)
 
         def stage_round(c):
             late = picked[:, PLANE_AT[2] + c * C : PLANE_AT[2] + (c + 2 * HOLD) * C]
@@ -176,7 +180,7 @@ def tile_list_sigm_mulP_kernel(
             )
 
         def stage_up(c):
-            quantize(x_codes, x_sc, x_bf, c, c + 1)
+            quantize(x_codes, x_sc, x_bf[:, wide(c)], c, c + 1)
             ga = psum2.tile([P, PACK, C], F32, name="ga")
             ub[c] = psum3.tile([P, PACK, C], F32, name="ub")
             cols = slice(c * C, (c + 1) * C)
@@ -191,38 +195,56 @@ def tile_list_sigm_mulP_kernel(
 
         def stage_glu(c):
             nc.vector.tensor_tensor(
-                h_bf[:, wide(c)].rearrange("p (j t) -> p j t", t=PACK),
+                h_bf[c // 2][:, wide(c % 2)].rearrange("p (j t) -> p j t", t=PACK),
                 ub[c][:].rearrange("p t j -> p j t"),
                 sig[c][:],
                 MULT,
             )
 
         def stage_down(c):
-            quantize(h_codes, h_sc, h_bf, c, c + 1)
             if c % 2 == 1:
+                quantize(h_codes, h_sc, h_bf[c // 2], c - 1, c + 1)
                 cols = slice((c - 1) * C, (c + 1) * C)
                 for u in range(2):
                     ysum[c - 1 + u] = psum3.tile([P, 2, 2 * C], F32, name="ysum")
                     for t in (2 * u, 2 * u + 1):
                         weights = wd_c[:, t * P : (t + 1) * P].bitcast(FP8X4)
                         product(ysum[c - 1 + u][:, t % 2, :], weights, 8, t, h_codes, h_sc, cols)
+                if 0 <= c // 2 - 1 < SIDE:
+                    side_gate(c // 2 - 1)
+                if c // 2 < SIDE:
+                    y_sb[c // 2] = keep.tile([P, 2, 2 * C], F32, name=f"y_sb{c // 2}")
+                    nc.scalar.copy(y_sb[c // 2][:], ysum[c - 1][:])
+
+        def results(n):
+            return res[n][:].rearrange("p (t j) -> p t j", t=PACK)
+
+        def gate_of(n):
+            half, j0 = divmod(2 * n * C, J // 2)
+            return gate[half][:, :, j0 : j0 + 2 * C]
+
+        def side_gate(n):
+            for t in range(2):
+                nc.gpsimd.tensor_tensor(results(n)[:, t, :], y_sb[n][:, t, :], gate_of(n)[:, t, :], MULT)
+            nc.sync.dma_start(out_rows[:, 0:2, 2 * n * C : 2 * (n + 1) * C], results(n)[:, 0:2, :])
 
         def stage_gate(c):
             n, u = divmod(c, 2)
             rows = slice(2 * u, 2 * u + 2)
-            if u == 0:
-                res[n] = keep.tile([P, PACK, 2 * C], F32, name=f"res{n}")
-            half, j0 = divmod(2 * n * C, J // 2)
-            nc.vector.tensor_tensor(res[n][:, rows, :], ysum[c][:], gate[half][:, rows, j0 : j0 + 2 * C], MULT)
-            nc.sync.dma_start(out_rows[:, rows, 2 * n * C : 2 * (n + 1) * C], res[n][:, rows, :])
+            if u == 1 or n >= SIDE:
+                nc.vector.tensor_tensor(results(n)[:, rows, :], ysum[c][:], gate_of(n)[:, rows, :], MULT)
+                nc.sync.dma_start(out_rows[:, rows, 2 * n * C : 2 * (n + 1) * C], results(n)[:, rows, :])
 
         def stage_yround(c):
             n, u = divmod(c, 2)
             copy = nc.vector.tensor_copy if c == CHUNKS - 1 else nc.scalar.copy
-            weave(y_bf[:, wide(c)], res[n][:, :, u * C : (u + 1) * C], copy)
+            cut = LAST_CUT if n == PAIRS - 1 else C
+            j0, j1 = ((0, cut), (cut, 2 * C))[u]
+            at = 2 * n * C
+            weave(y_bf[:, PACK * (at + j0) : PACK * (at + j1)], results(n)[:, :, j0:j1], copy)
             for c0, c1 in PLANE_GROUPS:
                 if c == c1 - 1:
-                    quantize(y_codes, y_sc, y_bf, c0, c1)
+                    quantize(y_codes, y_sc, y_bf[:, PACK * c0 * C : PACK * c1 * C], c0, c1)
                     nc.sync.dma_start(out_words[:, c0 * C : c1 * C], y_codes[:, c0 * C : c1 * C].bitcast(I32))
 
         stages = (stage_pick, stage_round, stage_up, stage_glu, stage_down, stage_gate, stage_yround)

@@ -30,7 +30,7 @@ PLANE_AT = (0, J, 2 * J, 2 * J + HOLD * C)
 EARLY_PICKS = (((0, FIRST), (FIRST, J)), ((0, 512), (512, J)), ((0, J),))
 EARLY_CUTS = ((0, 512), (512, 1024))
 PLANE_GROUPS = ((0, 4), (4, 6), (6, 8))
-LAG = (0, 1, 2, 4, 5, 8, 10)
+LAG = (0, 1, 2, 4, 5, 7, 9)
 LOAD_ORDER = (0, 1, 3, 2)
 GATE_CUTS = ((0, 512), (512, 1024))
 
@@ -61,7 +61,7 @@ def tile_list_sigm_mulP_kernel(
         x_bf = keep.tile([P, PACK * J], BF16, name="x_bf", align_bytes=64)
         res = [keep.tile([P, 2 * PACK * C], F32, name=f"res{n}", align_bytes=64) for n in range(PAIRS)]
         h_own = [keep.tile([P, 2 * PACK * C], BF16, name=f"h_own{n}", align_bytes=64) for n in range(PAIRS - SIDE)]
-        h_bf = [h_own[0][:]] + [res[n][:, : PACK * C].bitcast(BF16) for n in range(SIDE)] + [h[:] for h in h_own[1:]]
+        h_bf = [h_own[0][:]] + [res[n][:, 2 * C : 6 * C].bitcast(BF16) for n in range(SIDE)] + [h[:] for h in h_own[1:]]
         y_bf = keep.tile([P, PACK * J], BF16, name="y_bf", align_bytes=64)
         x_codes = keep.tile([P, J], U32, name="x_codes", align_bytes=64)
         h_codes = keep.tile([P, J], U32, name="h_codes", align_bytes=64)
@@ -224,8 +224,7 @@ def tile_list_sigm_mulP_kernel(
             return gate[half][:, :, j0 : j0 + 2 * C]
 
         def side_gate(n):
-            for t in range(2):
-                nc.gpsimd.tensor_tensor(results(n)[:, t, :], y_sb[n][:, t, :], gate_of(n)[:, t, :], MULT)
+            nc.gpsimd.tensor_tensor(results(n)[:, 0:2, :], y_sb[n][:], gate_of(n)[:, 0:2, :], MULT)
             nc.sync.dma_start(out_rows[:, 0:2, 2 * n * C : 2 * (n + 1) * C], results(n)[:, 0:2, :])
 
         def stage_gate(c):

@@ -1,6 +1,7 @@
 from contextlib import ExitStack
 
 import concourse.mybir as mybir
+from concourse.masks import make_identity
 
 K, R, N, T, J = 512, 512, 512, 2048, 1024
 FLOPS = 2 * J * (2 * K * R + R * N)
@@ -21,13 +22,12 @@ PACK = 4
 C = 128
 CHUNKS = J // C
 LANES = 16
-FIRST = 256
 HOLD = 3
 LAST_CUT = 80
 PAIRS = CHUNKS // 2
 SIDE = 2
 PLANE_AT = (0, J, 2 * J, 2 * J + HOLD * C)
-EARLY_PICKS = (((0, FIRST), (FIRST, J)), ((0, 512), (512, J)), ((0, J),))
+EARLY_PICKS = (((0, 128), (128, 384), (384, 768), (768, J)), ((0, 512), (512, J)), ((0, J),))
 EARLY_CUTS = ((0, 512), (512, 1024))
 PLANE_GROUPS = ((0, 4), (4, 6), (6, 8))
 LAG = (0, 1, 2, 4, 5, 7, 9)
@@ -70,6 +70,10 @@ def tile_list_sigm_mulP_kernel(
         h_sc = keep.tile([P, J], U8, name="h_sc", align_bytes=64)
         y_sc = keep.tile([P, J], U8, name="y_sc", align_bytes=64)
 
+        ident = keep.tile([P, P], F32, name="ident")
+        w_rows = keep.tile([P, C], F32, name="w_rows")
+        w_cols = keep.tile([P, J], F32, name="w_cols")
+
         x_rows = xT.rearrange("(p i) t -> p i t", i=PACK)
         g_rows = g.rearrange("(p t) j -> p t j", t=PACK)
         out_rows = out_0.rearrange("(p t) j -> p t j", t=PACK)
@@ -87,16 +91,15 @@ def tile_list_sigm_mulP_kernel(
                 )
 
         nc.vector.memset(w_sc_raw[:].bitcast(I32), 0)
+        nc.sync.dma_start(w_rows[:], wgt[0:P:8, :].rearrange("a (c x) -> a c x", x=C))
         nc.sync.dma_start(offsets[:], offs)
-        nc.sync.dma_start(weight[:, :FIRST], wgt[:, :FIRST])
         nc.sync.dma_start(wg_raw[:].bitcast(I32), wg_words[0].bitcast(I32))
         load_plane(0)
-        nc.sync.dma_start(weight[:, FIRST:], wgt[:, FIRST:])
-        load_scales(0, 3)
+        load_scales(0, 4)
         load_plane(1)
-        load_scales(3, 8)
+        load_scales(4, 9)
         load_plane(2)
-        load_scales(8, 12)
+        load_scales(9, 12)
         load_plane(3)
         nc.sync.dma_start(wu_raw[:].bitcast(I32), wu_words[0].rearrange("p r i -> p (r i)").bitcast(I32))
         nc.sync.dma_start(wd_raw[:].bitcast(I32), wd_words[0].rearrange("p n i -> p (n i)").bitcast(I32))
@@ -149,6 +152,22 @@ def tile_list_sigm_mulP_kernel(
 
         x_quads = x_bf[:].rearrange("p (j t) -> p j t", t=PACK)
         deal_bytes(wg_c[:], wg_raw[:], 2)
+        make_identity(nc, ident[:])
+        for copy, pieces in ((nc.scalar.copy, EARLY_PICKS[0][:2]), (nc.vector.tensor_copy, EARLY_PICKS[0][2:])):
+            turned = psum3.tile([P, P], F32, name="ysum")
+            nc.tensor.transpose(turned[:], w_rows[:], ident[:])
+            by_chunk = turned[:].rearrange("x (a c) -> x c a", c=CHUNKS)
+            for j0, j1 in pieces:
+                copy(
+                    w_cols[:, j0:j1].rearrange("x (c a r) -> x c a r", a=16, r=8),
+                    by_chunk[:, j0 // C : j1 // C, :].unsqueeze(3).broadcast_to([P, (j1 - j0) // C, 16, 8]),
+                )
+        for j0, j1 in EARLY_PICKS[0]:
+            spread = psum3.tile([P, j1 - j0], F32, name="ub")
+            for at in range(j0, j1, C):
+                nc.tensor.transpose(spread[:, at - j0 : at - j0 + C], w_cols[:, at : at + C], ident[:])
+            nc.scalar.copy(weight[:, j0:j1], spread[:])
+
         for n in range(3):
             for a, b in EARLY_PICKS[n]:
                 gather(LOAD_ORDER[n], a, b)

@@ -153,6 +153,8 @@ def tile_list_sigm_mulP_kernel(
         x_quads = x_bf[:].rearrange("p (j t) -> p j t", t=PACK)
         deal_bytes(wg_c[:], wg_raw[:], 2)
         make_identity(nc, ident[:])
+        warm = keep.tile([P, 1], F32, name="warm")
+        nc.scalar.activation(warm[:], ident[:, 0:1], SIGMOID)
         for copy, pieces in ((nc.scalar.copy, EARLY_PICKS[0][:2]), (nc.vector.tensor_copy, EARLY_PICKS[0][2:])):
             turned = psum3.tile([P, P], F32, name="ysum")
             nc.tensor.transpose(turned[:], w_rows[:], ident[:])

@@ -25,14 +25,19 @@ LANES = 16
 HOLD = 3
 LAST_CUT = 80
 PAIRS = CHUNKS // 2
-SIDE = 2
+SIDE = (0, 1)
+H_AT = (2, 0)
+SIG_HOLD = ()
+EARLY_GATES = 4
+EARLY_FROM = 2
+XROUND_V = ()
 PLANE_AT = (0, J, 2 * J, 2 * J + HOLD * C)
 EARLY_PICKS = (((0, 128), (128, 384), (384, 768), (768, J)), ((0, 512), (512, J)), ((0, J),))
 EARLY_CUTS = ((0, 512), (512, 1024))
-PLANE_GROUPS = ((0, 4), (4, 6), (6, 8))
-LAG = (0, 1, 2, 4, 5, 7, 9)
+PLANE_GROUPS = ((0, 2), (2, 4), (4, 6), (6, 8))
+LAG = (0, 1, 2, 4, 5, 6, 7, 11, 12)
+WORD_STORES = ((0, 4), (4, 6), (6, 8))
 LOAD_ORDER = (0, 1, 3, 2)
-GATE_CUTS = ((0, 512), (512, 1024))
 
 
 def tile_list_sigm_mulP_kernel(
@@ -56,12 +61,14 @@ def tile_list_sigm_mulP_kernel(
         wu_c = keep.tile([P, R], U32, name="wu_c", align_bytes=64)
         wd_c = keep.tile([P, N], U32, name="wd_c", align_bytes=64)
         w_sc = keep.tile([P, R], U8, name="w_sc", align_bytes=64)
-        gate = [keep.tile([P, PACK, b - a], F32, name=f"gate{a}") for a, b in GATE_CUTS]
+        gate_flat = [keep.tile([P, J], F32, name=f"gate{n}", align_bytes=64) for n in range(4)]
+        gate = [flat[:].rearrange("p (t j) -> p t j", t=2) for flat in gate_flat]
         picked = keep.tile([P, 3 * J + 2 * HOLD * C], F32, name="picked")
         x_bf = keep.tile([P, PACK * J], BF16, name="x_bf", align_bytes=64)
         res = [keep.tile([P, 2 * PACK * C], F32, name=f"res{n}", align_bytes=64) for n in range(PAIRS)]
-        h_own = [keep.tile([P, 2 * PACK * C], BF16, name=f"h_own{n}", align_bytes=64) for n in range(PAIRS - SIDE)]
-        h_bf = [h_own[0][:]] + [res[n][:, 2 * C : 6 * C].bitcast(BF16) for n in range(SIDE)] + [h[:] for h in h_own[1:]]
+        h_own = [keep.tile([P, 2 * PACK * C], BF16, name=f"h_own{n}", align_bytes=64) for n in range(PAIRS)]
+        h_bf = [res[n - 1][:, H_AT[n - 1] * C : (H_AT[n - 1] + 4) * C].bitcast(BF16) if n - 1 in SIDE else h_own[n][:] for n in range(PAIRS)]
+        h_bf[3] = gate_flat[1][:, 2 * C : 6 * C].bitcast(BF16)
         y_bf = keep.tile([P, PACK * J], BF16, name="y_bf", align_bytes=64)
         x_codes = keep.tile([P, J], U32, name="x_codes", align_bytes=64)
         h_codes = keep.tile([P, J], U32, name="h_codes", align_bytes=64)
@@ -103,8 +110,9 @@ def tile_list_sigm_mulP_kernel(
         load_plane(3)
         nc.sync.dma_start(wu_raw[:].bitcast(I32), wu_words[0].rearrange("p r i -> p (r i)").bitcast(I32))
         nc.sync.dma_start(wd_raw[:].bitcast(I32), wd_words[0].rearrange("p n i -> p (n i)").bitcast(I32))
-        for u, (a, b) in enumerate(GATE_CUTS):
-            nc.sync.dma_start(gate[u][:], g_rows[:, :, a:b])
+        for n in range(4):
+            half, u = divmod(n, 2)
+            nc.sync.dma_start(gate[n], g_rows[:, 2 * u : 2 * u + 2, half * J // 2 : (half + 1) * J // 2])
 
         def gather(i, j0, j1):
             nc.vector.tensor_tensor(
@@ -195,7 +203,8 @@ def tile_list_sigm_mulP_kernel(
 
         def stage_round(c):
             late = picked[:, PLANE_AT[2] + c * C : PLANE_AT[2] + (c + 2 * HOLD) * C]
-            nc.scalar.copy(
+            copy = nc.vector.tensor_copy if c in XROUND_V else nc.scalar.copy
+            copy(
                 x_quads[:, c * C : (c + 1) * C, 2:4],
                 late.rearrange("p (e x) -> p x e", e=2)[:, :C, :],
             )
@@ -209,7 +218,12 @@ def tile_list_sigm_mulP_kernel(
                 product(ga[:, t, :], wg_c[:, 2 * t * P : 2 * (t + 1) * P].bitcast(FP4X4), 0, t, x_codes, x_sc, cols)
             for t in range(PACK):
                 product(ub[c][:, t, :], wu_c[:, t * P : (t + 1) * P].bitcast(FP8X4), 4, t, x_codes, x_sc, cols)
-            sig[c] = ring.tile([P, C, PACK], F32, name="sig")
+            if c % 2 == 1 and c // 2 - 1 in SIG_HOLD:
+                sig[c] = res[c // 2 - 1][:, PACK * C :].rearrange("p (j t) -> p j t", t=PACK)
+            elif c == CHUNKS - 2:
+                sig[c] = y_bf[:, : 2 * PACK * C].bitcast(F32).rearrange("p (j t) -> p j t", t=PACK)
+            else:
+                sig[c] = ring.tile([P, C, PACK], F32, name="sig")
             nc.scalar.activation(sig[c][:], ga[:].rearrange("p t j -> p j t"), SIGMOID)
             if c == 1:
                 deal_words(wd_c, wd_raw)
@@ -231,28 +245,36 @@ def tile_list_sigm_mulP_kernel(
                     for t in (2 * u, 2 * u + 1):
                         weights = wd_c[:, t * P : (t + 1) * P].bitcast(FP8X4)
                         product(ysum[c - 1 + u][:, t % 2, :], weights, 8, t, h_codes, h_sc, cols)
-                if 0 <= c // 2 - 1 < SIDE:
+                if c // 2 - 1 in SIDE:
                     side_gate(c // 2 - 1)
-                if c // 2 < SIDE:
+                if c // 2 in SIDE:
                     y_sb[c // 2] = keep.tile([P, 2, 2 * C], F32, name=f"y_sb{c // 2}")
                     nc.scalar.copy(y_sb[c // 2][:], ysum[c - 1][:])
 
         def results(n):
             return res[n][:].rearrange("p (t j) -> p t j", t=PACK)
 
-        def gate_of(n):
+        def gate_of(n, u):
             half, j0 = divmod(2 * n * C, J // 2)
-            return gate[half][:, :, j0 : j0 + 2 * C]
+            return gate[2 * half + u][:, :, j0 : j0 + 2 * C]
 
         def side_gate(n):
-            nc.gpsimd.tensor_tensor(results(n)[:, 0:2, :], y_sb[n][:], gate_of(n)[:, 0:2, :], MULT)
+            nc.gpsimd.tensor_tensor(results(n)[:, 0:2, :], y_sb[n][:], gate_of(n, 0), MULT)
             nc.sync.dma_start(out_rows[:, 0:2, 2 * n * C : 2 * (n + 1) * C], results(n)[:, 0:2, :])
 
+        def stage_gate_early(c):
+            if EARLY_FROM <= c < EARLY_GATES:
+                gate_unit(c)
+
         def stage_gate(c):
+            if not EARLY_FROM <= c < EARLY_GATES:
+                gate_unit(c)
+
+        def gate_unit(c):
             n, u = divmod(c, 2)
             rows = slice(2 * u, 2 * u + 2)
-            if u == 1 or n >= SIDE:
-                nc.vector.tensor_tensor(results(n)[:, rows, :], ysum[c][:], gate_of(n)[:, rows, :], MULT)
+            if u == 1 or n not in SIDE:
+                nc.vector.tensor_tensor(results(n)[:, rows, :], ysum[c][:], gate_of(n, u), MULT)
                 nc.sync.dma_start(out_rows[:, rows, 2 * n * C : 2 * (n + 1) * C], results(n)[:, rows, :])
 
         def stage_yround(c):
@@ -262,12 +284,16 @@ def tile_list_sigm_mulP_kernel(
             j0, j1 = ((0, cut), (cut, 2 * C))[u]
             at = 2 * n * C
             weave(y_bf[:, PACK * (at + j0) : PACK * (at + j1)], results(n)[:, :, j0:j1], copy)
+
+        def stage_planes(c):
             for c0, c1 in PLANE_GROUPS:
                 if c == c1 - 1:
                     quantize(y_codes, y_sc, y_bf[:, PACK * c0 * C : PACK * c1 * C], c0, c1)
+            for c0, c1 in WORD_STORES:
+                if c == c1 - 1:
                     nc.sync.dma_start(out_words[:, c0 * C : c1 * C], y_codes[:, c0 * C : c1 * C].bitcast(I32))
 
-        stages = (stage_pick, stage_round, stage_up, stage_glu, stage_down, stage_gate, stage_yround)
+        stages = (stage_pick, stage_round, stage_up, stage_glu, stage_down, stage_gate_early, stage_gate, stage_yround, stage_planes)
         for step in range(CHUNKS + LAG[-1]):
             for stage, lag in zip(stages, LAG):
                 if 0 <= step - lag < CHUNKS:

@@ -18,26 +18,22 @@ MULT = mybir.AluOpType.mult
 SIGMOID = mybir.ActivationFunctionType.Sigmoid
 
 P = 128
-PACK = 4
+SLOTS = 4
 C = 128
 CHUNKS = J // C
-LANES = 16
-HOLD = 3
-LAST_CUT = 80
 PAIRS = CHUNKS // 2
-SIDE = (0, 1)
-H_AT = (2, 0)
-SIG_HOLD = ()
-EARLY_GATES = 4
-EARLY_FROM = 2
-XROUND_V = ()
-PLANE_AT = (0, J, 2 * J, 2 * J + HOLD * C)
-EARLY_PICKS = (((0, 128), (128, 384), (384, 768), (768, J)), ((0, 512), (512, J)), ((0, J),))
-EARLY_CUTS = ((0, 512), (512, 1024))
-PLANE_GROUPS = ((0, 2), (2, 4), (4, 6), (6, 8))
-LAG = (0, 1, 2, 4, 5, 6, 7, 11, 12)
-WORD_STORES = ((0, 4), (4, 6), (6, 8))
+LANES = 16
+
 LOAD_ORDER = (0, 1, 3, 2)
+FIRST_PICKS = (((0, 128), (128, 384), (384, 768), (768, J)), ((0, J // 2), (J // 2, J)), ((0, J),))
+AHEAD = 3
+PICKS_AT = (0, J, 2 * J, 2 * J + AHEAD * C)
+SCALE_LOADS = ((0, 4), (4, 9), (9, 12))
+WG_ROWS, WU_ROWS, WD_ROWS = 0, 4, 8
+ROUND_LAG, UP_LAG, GLU_LAG, DOWN_LAG = 1, 2, 4, 5
+SIDE_PAIRS = 2
+LAST_CUT = 80
+WORD_STORES = ((0, 4), (4, 6), (6, 8))
 
 
 def tile_list_sigm_mulP_kernel(
@@ -52,24 +48,28 @@ def tile_list_sigm_mulP_kernel(
 
         offsets = keep.tile([P, J // LANES], U16, name="offsets")
         weight = keep.tile([P, J], F32, name="weight")
-        plane = [keep.tile([P, T], F32, name=f"plane{i}") for i in range(PACK)]
+        x_slot = [keep.tile([P, T], F32, name=f"x_slot{t}") for t in range(SLOTS)]
         wg_raw = keep.tile([P, 2 * R], U8, name="wg_raw", align_bytes=64)
         wu_raw = keep.tile([P, R], U32, name="wu_raw", align_bytes=64)
         wd_raw = keep.tile([P, N], U32, name="wd_raw", align_bytes=64)
         w_sc_raw = keep.tile([P, R], U8, name="w_sc_raw", align_bytes=64)
-        wg_c = keep.tile([P, 2 * R], U8, name="wg_c", align_bytes=64)
-        wu_c = keep.tile([P, R], U32, name="wu_c", align_bytes=64)
-        wd_c = keep.tile([P, N], U32, name="wd_c", align_bytes=64)
+        wg_dealt = keep.tile([P, 2 * R], U8, name="wg_dealt", align_bytes=64)
+        wu_dealt = keep.tile([P, R], U32, name="wu_dealt", align_bytes=64)
+        wd_dealt = keep.tile([P, N], U32, name="wd_dealt", align_bytes=64)
         w_sc = keep.tile([P, R], U8, name="w_sc", align_bytes=64)
-        gate_flat = [keep.tile([P, J], F32, name=f"gate{n}", align_bytes=64) for n in range(4)]
-        gate = [flat[:].rearrange("p (t j) -> p t j", t=2) for flat in gate_flat]
-        picked = keep.tile([P, 3 * J + 2 * HOLD * C], F32, name="picked")
-        x_bf = keep.tile([P, PACK * J], BF16, name="x_bf", align_bytes=64)
-        res = [keep.tile([P, 2 * PACK * C], F32, name=f"res{n}", align_bytes=64) for n in range(PAIRS)]
-        h_own = [keep.tile([P, 2 * PACK * C], BF16, name=f"h_own{n}", align_bytes=64) for n in range(PAIRS)]
-        h_bf = [res[n - 1][:, H_AT[n - 1] * C : (H_AT[n - 1] + 4) * C].bitcast(BF16) if n - 1 in SIDE else h_own[n][:] for n in range(PAIRS)]
-        h_bf[3] = gate_flat[1][:, 2 * C : 6 * C].bitcast(BF16)
-        y_bf = keep.tile([P, PACK * J], BF16, name="y_bf", align_bytes=64)
+        g_flat = [keep.tile([P, J], F32, name=f"g{n}", align_bytes=64) for n in range(4)]
+        g_part = [flat[:].rearrange("p (t j) -> p t j", t=2) for flat in g_flat]
+        picked = keep.tile([P, 3 * J + 2 * AHEAD * C], F32, name="picked")
+        x_bf = keep.tile([P, SLOTS * J], BF16, name="x_bf", align_bytes=64)
+        res = [keep.tile([P, 2 * SLOTS * C], F32, name=f"res{n}", align_bytes=64) for n in range(PAIRS)]
+        h_first = keep.tile([P, 2 * SLOTS * C], BF16, name="h_first", align_bytes=64)
+        h_bf = [
+            h_first[:],
+            res[0][:, 2 * C : 6 * C].bitcast(BF16),
+            res[1][:, : 4 * C].bitcast(BF16),
+            g_flat[1][:, 2 * C : 6 * C].bitcast(BF16),
+        ]
+        y_bf = keep.tile([P, SLOTS * J], BF16, name="y_bf", align_bytes=64)
         x_codes = keep.tile([P, J], U32, name="x_codes", align_bytes=64)
         h_codes = keep.tile([P, J], U32, name="h_codes", align_bytes=64)
         y_codes = keep.tile([P, J], U32, name="y_codes", align_bytes=64)
@@ -81,15 +81,12 @@ def tile_list_sigm_mulP_kernel(
         w_rows = keep.tile([P, C], F32, name="w_rows")
         w_cols = keep.tile([P, J], F32, name="w_cols")
 
-        x_rows = xT.rearrange("(p i) t -> p i t", i=PACK)
-        g_rows = g.rearrange("(p t) j -> p t j", t=PACK)
-        out_rows = out_0.rearrange("(p t) j -> p t j", t=PACK)
-        out_words = out_1[0].rearrange("p j i -> p (j i)").bitcast(I32)
+        x_rows = xT.rearrange("(p t) i -> p t i", t=SLOTS)
+        g_rows = g.rearrange("(p t) j -> p t j", t=SLOTS)
+        out_rows = out_0.rearrange("(p t) j -> p t j", t=SLOTS)
+        out_words = out_1[0].rearrange("p j t -> p (j t)").bitcast(I32)
 
-        def load_plane(n):
-            nc.sync.dma_start(plane[LOAD_ORDER[n]][:], x_rows[:, LOAD_ORDER[n], :])
-
-        def load_scales(first, last):
+        def load_scale_rows(first, last):
             for n in range(first, last):
                 a, q = divmod(n, 4)
                 nc.sync.dma_start(
@@ -101,43 +98,34 @@ def tile_list_sigm_mulP_kernel(
         nc.sync.dma_start(w_rows[:], wgt[0:P:8, :].rearrange("a (c x) -> a c x", x=C))
         nc.sync.dma_start(offsets[:], offs)
         nc.sync.dma_start(wg_raw[:].bitcast(I32), wg_words[0].bitcast(I32))
-        load_plane(0)
-        load_scales(0, 4)
-        load_plane(1)
-        load_scales(4, 9)
-        load_plane(2)
-        load_scales(9, 12)
-        load_plane(3)
-        nc.sync.dma_start(wu_raw[:].bitcast(I32), wu_words[0].rearrange("p r i -> p (r i)").bitcast(I32))
-        nc.sync.dma_start(wd_raw[:].bitcast(I32), wd_words[0].rearrange("p n i -> p (n i)").bitcast(I32))
+        for n, t in enumerate(LOAD_ORDER):
+            nc.sync.dma_start(x_slot[t][:], x_rows[:, t, :])
+            if n < len(SCALE_LOADS):
+                load_scale_rows(*SCALE_LOADS[n])
+        nc.sync.dma_start(wu_raw[:].bitcast(I32), wu_words[0].rearrange("p r t -> p (r t)").bitcast(I32))
+        nc.sync.dma_start(wd_raw[:].bitcast(I32), wd_words[0].rearrange("p n t -> p (n t)").bitcast(I32))
         for n in range(4):
             half, u = divmod(n, 2)
-            nc.sync.dma_start(gate[n], g_rows[:, 2 * u : 2 * u + 2, half * J // 2 : (half + 1) * J // 2])
+            nc.sync.dma_start(g_part[n], g_rows[:, 2 * u : 2 * u + 2, half * J // 2 : (half + 1) * J // 2])
 
-        def gather(i, j0, j1):
+        def gather(t, j0, j1):
             nc.vector.tensor_tensor(
-                picked[:, PLANE_AT[i] + j0 : PLANE_AT[i] + j1],
-                plane[i][:].indirect(offsets[:, j0 // LANES : j1 // LANES]),
+                picked[:, PICKS_AT[t] + j0 : PICKS_AT[t] + j1],
+                x_slot[t][:].indirect(offsets[:, j0 // LANES : j1 // LANES]),
                 weight[:, j0:j1],
                 MULT,
             )
 
         def deal_bytes(dst, src, width):
             nc.vector.tensor_copy(
-                dst.rearrange("p (t m b) -> p t m b", t=PACK, b=width),
-                src.rearrange("p (m t b) -> p t m b", t=PACK, b=width),
+                dst.rearrange("p (t m b) -> p t m b", t=SLOTS, b=width),
+                src.rearrange("p (m t b) -> p t m b", t=SLOTS, b=width),
             )
 
         def deal_words(dst, src):
             nc.vector.tensor_copy(
-                dst[:].bitcast(I32).rearrange("p (t m i) -> p m t i", t=PACK, i=4),
-                src[:].bitcast(I32).rearrange("p (m i t) -> p m t i", t=PACK, i=4),
-            )
-
-        def weave(dst, src, copy):
-            copy(
-                dst.rearrange("p (c i t) -> p c t i", i=2, t=PACK),
-                src.rearrange("p t (c i) -> p c t i", i=2),
+                dst[:].bitcast(I32).rearrange("p (t m i) -> p m t i", t=SLOTS, i=4),
+                src[:].bitcast(I32).rearrange("p (m i t) -> p m t i", t=SLOTS, i=4),
             )
 
         def quantize(codes, scales, src, c0, c1):
@@ -147,157 +135,157 @@ def tile_list_sigm_mulP_kernel(
                 in_=src,
             )
 
-        def product(acc, weights, first_row, t, codes, scales, cols):
+        def product(acc, weights, scale_rows, t, codes, scales, cols):
             nc.tensor.matmul_mx(
                 out=acc,
                 lhsT=weights,
-                lhsT_scale=w_sc[first_row:, t * P : (t + 1) * P],
+                lhsT_scale=w_sc[scale_rows:, t * P : (t + 1) * P],
                 rhs=codes[:, cols].bitcast(FP8X4),
                 rhs_scale=scales[:, cols],
                 start=True,
                 stop=True,
             )
 
-        x_quads = x_bf[:].rearrange("p (j t) -> p j t", t=PACK)
-        deal_bytes(wg_c[:], wg_raw[:], 2)
+        x_quads = x_bf[:].rearrange("p (j t) -> p j t", t=SLOTS)
+        deal_bytes(wg_dealt[:], wg_raw[:], 2)
         make_identity(nc, ident[:])
         warm = keep.tile([P, 1], F32, name="warm")
         nc.scalar.activation(warm[:], ident[:, 0:1], SIGMOID)
-        for copy, pieces in ((nc.scalar.copy, EARLY_PICKS[0][:2]), (nc.vector.tensor_copy, EARLY_PICKS[0][2:])):
+
+        pieces = FIRST_PICKS[0]
+        for copy, share in ((nc.scalar.copy, pieces[:2]), (nc.vector.tensor_copy, pieces[2:])):
             turned = psum3.tile([P, P], F32, name="ysum")
             nc.tensor.transpose(turned[:], w_rows[:], ident[:])
             by_chunk = turned[:].rearrange("x (a c) -> x c a", c=CHUNKS)
-            for j0, j1 in pieces:
+            for j0, j1 in share:
                 copy(
                     w_cols[:, j0:j1].rearrange("x (c a r) -> x c a r", a=16, r=8),
                     by_chunk[:, j0 // C : j1 // C, :].unsqueeze(3).broadcast_to([P, (j1 - j0) // C, 16, 8]),
                 )
-        for j0, j1 in EARLY_PICKS[0]:
+        for j0, j1 in pieces:
             spread = psum3.tile([P, j1 - j0], F32, name="ub")
             for at in range(j0, j1, C):
                 nc.tensor.transpose(spread[:, at - j0 : at - j0 + C], w_cols[:, at : at + C], ident[:])
             nc.scalar.copy(weight[:, j0:j1], spread[:])
 
-        for n in range(3):
-            for a, b in EARLY_PICKS[n]:
-                gather(LOAD_ORDER[n], a, b)
-            if n == 2:
-                deal_bytes(w_sc[:], w_sc_raw[:], 1)
-            if n == 1:
-                early = picked[:, : 2 * J].rearrange("p (e j) -> p j e", e=2)
-                for a, b in EARLY_CUTS:
-                    nc.scalar.copy(x_quads[:, a:b, 0:2], early[:, a:b, :])
+        for j0, j1 in FIRST_PICKS[0]:
+            gather(LOAD_ORDER[0], j0, j1)
+        for j0, j1 in FIRST_PICKS[1]:
+            gather(LOAD_ORDER[1], j0, j1)
+        low_slots = picked[:, : 2 * J].rearrange("p (t j) -> p j t", t=2)
+        for j0, j1 in FIRST_PICKS[1]:
+            nc.scalar.copy(x_quads[:, j0:j1, 0:2], low_slots[:, j0:j1, :])
+        for j0, j1 in FIRST_PICKS[2]:
+            gather(LOAD_ORDER[2], j0, j1)
+        deal_bytes(w_sc[:], w_sc_raw[:], 1)
 
         sig = {}
         ub = {}
         ysum = {}
-        y_sb = {}
+        y_copy = {}
 
         def wide(c):
-            return slice(PACK * c * C, PACK * (c + 1) * C)
+            return slice(SLOTS * c * C, SLOTS * (c + 1) * C)
 
-        def stage_pick(c):
+        def results(n):
+            return res[n][:].rearrange("p (t j) -> p t j", t=SLOTS)
+
+        def g_of(n, u):
+            half, j0 = divmod(2 * n * C, J // 2)
+            return g_part[2 * half + u][:, :, j0 : j0 + 2 * C]
+
+        def store(n, u):
+            slots = slice(2 * u, 2 * u + 2)
+            nc.sync.dma_start(out_rows[:, slots, 2 * n * C : 2 * (n + 1) * C], results(n)[:, slots, :])
+
+        def pick(c):
             gather(LOAD_ORDER[3], c * C, (c + 1) * C)
             if c == 1:
-                deal_words(wu_c, wu_raw)
+                deal_words(wu_dealt, wu_raw)
 
-        def stage_round(c):
-            late = picked[:, PLANE_AT[2] + c * C : PLANE_AT[2] + (c + 2 * HOLD) * C]
-            copy = nc.vector.tensor_copy if c in XROUND_V else nc.scalar.copy
-            copy(
+        def round_x(c):
+            high_slots = picked[:, PICKS_AT[2] + c * C : PICKS_AT[2] + (c + 2 * AHEAD) * C]
+            nc.scalar.copy(
                 x_quads[:, c * C : (c + 1) * C, 2:4],
-                late.rearrange("p (e x) -> p x e", e=2)[:, :C, :],
+                high_slots.rearrange("p (t x) -> p x t", t=2)[:, :C, :],
             )
 
-        def stage_up(c):
+        def up(c):
             quantize(x_codes, x_sc, x_bf[:, wide(c)], c, c + 1)
-            ga = psum2.tile([P, PACK, C], F32, name="ga")
-            ub[c] = psum3.tile([P, PACK, C], F32, name="ub")
+            ga = psum2.tile([P, SLOTS, C], F32, name="ga")
+            ub[c] = psum3.tile([P, SLOTS, C], F32, name="ub")
             cols = slice(c * C, (c + 1) * C)
-            for t in range(PACK):
-                product(ga[:, t, :], wg_c[:, 2 * t * P : 2 * (t + 1) * P].bitcast(FP4X4), 0, t, x_codes, x_sc, cols)
-            for t in range(PACK):
-                product(ub[c][:, t, :], wu_c[:, t * P : (t + 1) * P].bitcast(FP8X4), 4, t, x_codes, x_sc, cols)
-            if c % 2 == 1 and c // 2 - 1 in SIG_HOLD:
-                sig[c] = res[c // 2 - 1][:, PACK * C :].rearrange("p (j t) -> p j t", t=PACK)
-            elif c == CHUNKS - 2:
-                sig[c] = y_bf[:, : 2 * PACK * C].bitcast(F32).rearrange("p (j t) -> p j t", t=PACK)
+            for t in range(SLOTS):
+                weights = wg_dealt[:, 2 * t * P : 2 * (t + 1) * P].bitcast(FP4X4)
+                product(ga[:, t, :], weights, WG_ROWS, t, x_codes, x_sc, cols)
+            for t in range(SLOTS):
+                weights = wu_dealt[:, t * P : (t + 1) * P].bitcast(FP8X4)
+                product(ub[c][:, t, :], weights, WU_ROWS, t, x_codes, x_sc, cols)
+            if c == CHUNKS - 2:
+                sig[c] = y_bf[:, : 2 * SLOTS * C].bitcast(F32).rearrange("p (j t) -> p j t", t=SLOTS)
             else:
-                sig[c] = ring.tile([P, C, PACK], F32, name="sig")
+                sig[c] = ring.tile([P, C, SLOTS], F32, name="sig")
             nc.scalar.activation(sig[c][:], ga[:].rearrange("p t j -> p j t"), SIGMOID)
             if c == 1:
-                deal_words(wd_c, wd_raw)
+                deal_words(wd_dealt, wd_raw)
 
-        def stage_glu(c):
+        def glu(c):
             nc.vector.tensor_tensor(
-                h_bf[c // 2][:, wide(c % 2)].rearrange("p (j t) -> p j t", t=PACK),
+                h_bf[c // 2][:, wide(c % 2)].rearrange("p (j t) -> p j t", t=SLOTS),
                 ub[c][:].rearrange("p t j -> p j t"),
                 sig[c][:],
                 MULT,
             )
 
-        def stage_down(c):
-            if c % 2 == 1:
-                quantize(h_codes, h_sc, h_bf[c // 2], c - 1, c + 1)
-                cols = slice((c - 1) * C, (c + 1) * C)
-                for u in range(2):
-                    ysum[c - 1 + u] = psum3.tile([P, 2, 2 * C], F32, name="ysum")
-                    for t in (2 * u, 2 * u + 1):
-                        weights = wd_c[:, t * P : (t + 1) * P].bitcast(FP8X4)
-                        product(ysum[c - 1 + u][:, t % 2, :], weights, 8, t, h_codes, h_sc, cols)
-                if c // 2 - 1 in SIDE:
-                    side_gate(c // 2 - 1)
-                if c // 2 in SIDE:
-                    y_sb[c // 2] = keep.tile([P, 2, 2 * C], F32, name=f"y_sb{c // 2}")
-                    nc.scalar.copy(y_sb[c // 2][:], ysum[c - 1][:])
+        def down(n):
+            quantize(h_codes, h_sc, h_bf[n], 2 * n, 2 * n + 2)
+            cols = slice(2 * n * C, 2 * (n + 1) * C)
+            for u in range(2):
+                ysum[n, u] = psum3.tile([P, 2, 2 * C], F32, name="ysum")
+                for t in (2 * u, 2 * u + 1):
+                    weights = wd_dealt[:, t * P : (t + 1) * P].bitcast(FP8X4)
+                    product(ysum[n, u][:, t % 2, :], weights, WD_ROWS, t, h_codes, h_sc, cols)
+            if 1 <= n <= SIDE_PAIRS:
+                nc.gpsimd.tensor_tensor(results(n - 1)[:, 0:2, :], y_copy[n - 1][:], g_of(n - 1, 0), MULT)
+                store(n - 1, 0)
+            if n < SIDE_PAIRS:
+                y_copy[n] = keep.tile([P, 2, 2 * C], F32, name=f"y_copy{n}")
+                nc.scalar.copy(y_copy[n][:], ysum[n, 0][:])
 
-        def results(n):
-            return res[n][:].rearrange("p (t j) -> p t j", t=PACK)
+        def gate(n, u):
+            nc.vector.tensor_tensor(results(n)[:, 2 * u : 2 * u + 2, :], ysum[n, u][:], g_of(n, u), MULT)
+            store(n, u)
 
-        def gate_of(n, u):
-            half, j0 = divmod(2 * n * C, J // 2)
-            return gate[2 * half + u][:, :, j0 : j0 + 2 * C]
+        gates = {}
+        for n in range(PAIRS):
+            if n >= SIDE_PAIRS:
+                gates[DOWN_LAG + 2 * n + 2] = (n, 0)
+            gates[DOWN_LAG + 2 * n + (2 if n == 1 else 3)] = (n, 1)
 
-        def side_gate(n):
-            nc.gpsimd.tensor_tensor(results(n)[:, 0:2, :], y_sb[n][:], gate_of(n, 0), MULT)
-            nc.sync.dma_start(out_rows[:, 0:2, 2 * n * C : 2 * (n + 1) * C], results(n)[:, 0:2, :])
-
-        def stage_gate_early(c):
-            if EARLY_FROM <= c < EARLY_GATES:
-                gate_unit(c)
-
-        def stage_gate(c):
-            if not EARLY_FROM <= c < EARLY_GATES:
-                gate_unit(c)
-
-        def gate_unit(c):
-            n, u = divmod(c, 2)
-            rows = slice(2 * u, 2 * u + 2)
-            if u == 1 or n not in SIDE:
-                nc.vector.tensor_tensor(results(n)[:, rows, :], ysum[c][:], gate_of(n, u), MULT)
-                nc.sync.dma_start(out_rows[:, rows, 2 * n * C : 2 * (n + 1) * C], results(n)[:, rows, :])
-
-        def stage_yround(c):
-            n, u = divmod(c, 2)
-            copy = nc.vector.tensor_copy if c == CHUNKS - 1 else nc.scalar.copy
-            cut = LAST_CUT if n == PAIRS - 1 else C
-            j0, j1 = ((0, cut), (cut, 2 * C))[u]
-            at = 2 * n * C
-            weave(y_bf[:, PACK * (at + j0) : PACK * (at + j1)], results(n)[:, :, j0:j1], copy)
-
-        def stage_planes(c):
-            for c0, c1 in PLANE_GROUPS:
-                if c == c1 - 1:
-                    quantize(y_codes, y_sc, y_bf[:, PACK * c0 * C : PACK * c1 * C], c0, c1)
-            for c0, c1 in WORD_STORES:
-                if c == c1 - 1:
-                    nc.sync.dma_start(out_words[:, c0 * C : c1 * C], y_codes[:, c0 * C : c1 * C].bitcast(I32))
-
-        stages = (stage_pick, stage_round, stage_up, stage_glu, stage_down, stage_gate_early, stage_gate, stage_yround, stage_planes)
-        for step in range(CHUNKS + LAG[-1]):
-            for stage, lag in zip(stages, LAG):
+        for step in range(max(gates) + 1):
+            for stage, lag in ((pick, 0), (round_x, ROUND_LAG), (up, UP_LAG), (glu, GLU_LAG)):
                 if 0 <= step - lag < CHUNKS:
                     stage(step - lag)
+            n, u = divmod(step - DOWN_LAG, 2)
+            if u == 1 and 0 <= n < PAIRS:
+                down(n)
+            if step in gates:
+                gate(*gates[step])
+
+        for n in range(PAIRS):
+            last = n == PAIRS - 1
+            cut = LAST_CUT if last else C
+            second = nc.vector.tensor_copy if last else nc.scalar.copy
+            for j0, j1, copy in ((0, cut, nc.scalar.copy), (cut, 2 * C, second)):
+                dst = y_bf[:, SLOTS * (2 * n * C + j0) : SLOTS * (2 * n * C + j1)]
+                copy(
+                    dst.rearrange("p (c i t) -> p c t i", i=2, t=SLOTS),
+                    results(n)[:, :, j0:j1].rearrange("p t (c i) -> p c t i", i=2),
+                )
+            quantize(y_codes, y_sc, y_bf[:, 2 * n * SLOTS * C : 2 * (n + 1) * SLOTS * C], 2 * n, 2 * n + 2)
+            for c0, c1 in WORD_STORES:
+                if c1 == 2 * n + 2:
+                    nc.sync.dma_start(out_words[:, c0 * C : c1 * C], y_codes[:, c0 * C : c1 * C].bitcast(I32))
 
         for q in range(4):
             queue = nc.scalar if q % 2 else nc.sync

@@ -26,8 +26,10 @@ LANES = 16
 
 LOAD_ORDER = (0, 1, 3, 2)
 FIRST_PICKS = (((0, 128), (128, 384), (384, 768), (768, J)), ((0, J // 2), (J // 2, J)), ((0, J),))
-AHEAD = 3
-PICKS_AT = (0, J, 2 * J, 2 * J + AHEAD * C)
+X_PARTS = ((0, 5 * C), (5 * C, J))
+FREE = 4
+PICKS_AT = (0, J, 2 * J, 2 * J + FREE * C)
+AFTER = {4: 0, 5: 4, 6: 4, 7: 3}
 SCALE_LOADS = ((0, 4), (4, 9), (9, 12))
 WG_ROWS, WU_ROWS, WD_ROWS = 0, 4, 8
 ROUND_LAG, UP_LAG, GLU_LAG, DOWN_LAG = 1, 2, 4, 5
@@ -55,19 +57,35 @@ def tile_list_sigm_mulP_kernel(
         w_sc_raw = keep.tile([P, R], U8, name="w_sc_raw", align_bytes=64)
         wg_dealt = keep.tile([P, 2 * R], U8, name="wg_dealt", align_bytes=64)
         wu_dealt = keep.tile([P, R], U32, name="wu_dealt", align_bytes=64)
-        wd_dealt = keep.tile([P, N], U32, name="wd_dealt", align_bytes=64)
-        w_sc = keep.tile([P, R], U8, name="w_sc", align_bytes=64)
-        g_flat = [keep.tile([P, J], F32, name=f"g{n}", align_bytes=64) for n in range(4)]
-        g_part = [flat[:].rearrange("p (t j) -> p t j", t=2) for flat in g_flat]
-        picked = keep.tile([P, 3 * J + 2 * AHEAD * C], F32, name="picked")
-        x_bf = keep.tile([P, SLOTS * J], BF16, name="x_bf", align_bytes=64)
-        res = [keep.tile([P, 2 * SLOTS * C], F32, name=f"res{n}", align_bytes=64) for n in range(PAIRS)]
+        weight_first = keep.tile([P, C], F32, name="weight_first", align_bytes=64)
+        w_sc = keep.tile([P, R], U8, name="w_sc", tag="weight_first", align_bytes=64)
+        g_low = keep.tile([P, 2, 4 * C], F32, name="g_low", align_bytes=64)
+        g_then_res = keep.tile([P, 6 * 2 * C], F32, name="g_then_res", align_bytes=64)
+        g_second = keep.tile([P, 2 * 2 * C], F32, name="g_second", align_bytes=64)
+        g_late = keep.tile([P, SLOTS, 4 * C], F32, name="g_late", align_bytes=64)
+        g_part = {
+            (0, 1): g_then_res[:, : 4 * C].rearrange("p (t j) -> p t j", t=2),
+            (1, 1): g_second[:].rearrange("p (t j) -> p t j", t=2),
+        }
+        for n in range(2):
+            g_part[n, 0] = g_low[:, :, 2 * n * C : 2 * (n + 1) * C]
+            for u in range(2):
+                g_part[2 + n, u] = g_late[:, 2 * u : 2 * u + 2, 2 * n * C : 2 * (n + 1) * C]
+        picked = keep.tile([P, 2 * J + 18 * C], F32, name="picked")
+        x_bf = [
+            keep.tile([P, SLOTS * (j1 - j0)], BF16, name=f"x_bf{j0}", align_bytes=64) for j0, j1 in X_PARTS
+        ]
+        res = [
+            g_then_res[:, 4 * C :] if n == 1 else keep.tile([P, 2 * SLOTS * C], F32, name=f"res{n}", align_bytes=64)[:]
+            for n in range(PAIRS)
+        ]
+        wd_dealt = keep.tile([P, N], U32, name="wd_dealt", tag="x_bf0", align_bytes=64)
         h_first = keep.tile([P, 2 * SLOTS * C], BF16, name="h_first", align_bytes=64)
         h_bf = [
             h_first[:],
-            res[0][:, 2 * C : 6 * C].bitcast(BF16),
-            res[1][:, : 4 * C].bitcast(BF16),
-            g_flat[1][:, 2 * C : 6 * C].bitcast(BF16),
+            res[0][:, : 4 * C].bitcast(BF16),
+            g_then_res[:, 2 * C : 6 * C].bitcast(BF16),
+            g_second[:].bitcast(BF16),
         ]
         y_bf = keep.tile([P, SLOTS * J], BF16, name="y_bf", align_bytes=64)
         x_codes = keep.tile([P, J], U32, name="x_codes", align_bytes=64)
@@ -102,17 +120,19 @@ def tile_list_sigm_mulP_kernel(
             nc.sync.dma_start(x_slot[t][:], x_rows[:, t, :])
             if n < len(SCALE_LOADS):
                 load_scale_rows(*SCALE_LOADS[n])
-        nc.sync.dma_start(wu_raw[:].bitcast(I32), wu_words[0].rearrange("p r t -> p (r t)").bitcast(I32))
         nc.sync.dma_start(wd_raw[:].bitcast(I32), wd_words[0].rearrange("p n t -> p (n t)").bitcast(I32))
-        for n in range(4):
-            half, u = divmod(n, 2)
-            nc.sync.dma_start(g_part[n], g_rows[:, 2 * u : 2 * u + 2, half * J // 2 : (half + 1) * J // 2])
+        nc.sync.dma_start(wu_raw[:].bitcast(I32), wu_words[0].rearrange("p r t -> p (r t)").bitcast(I32))
+        nc.sync.dma_start(g_part[0, 1], g_rows[:, 2:4, : 2 * C])
+        nc.sync.dma_start(g_low[:], g_rows[:, 0:2, : 4 * C])
+        nc.sync.dma_start(g_part[1, 1], g_rows[:, 2:4, 2 * C : 4 * C])
+        nc.sync.dma_start(g_late[:], g_rows[:, :, 4 * C :])
 
-        def gather(t, j0, j1):
+        def gather(t, j0, j1, at=None):
+            at = PICKS_AT[t] + j0 if at is None else at
             nc.vector.tensor_tensor(
-                picked[:, PICKS_AT[t] + j0 : PICKS_AT[t] + j1],
+                picked[:, at : at + j1 - j0],
                 x_slot[t][:].indirect(offsets[:, j0 // LANES : j1 // LANES]),
-                weight[:, j0:j1],
+                weight_first[:] if (t, j0) == (LOAD_ORDER[3], 0) else weight[:, j0:j1],
                 MULT,
             )
 
@@ -122,8 +142,8 @@ def tile_list_sigm_mulP_kernel(
                 src.rearrange("p (m t b) -> p t m b", t=SLOTS, b=width),
             )
 
-        def deal_words(dst, src):
-            nc.vector.tensor_copy(
+        def deal_words(dst, src, engine=nc.vector):
+            engine.tensor_copy(
                 dst[:].bitcast(I32).rearrange("p (t m i) -> p m t i", t=SLOTS, i=4),
                 src[:].bitcast(I32).rearrange("p (m i t) -> p m t i", t=SLOTS, i=4),
             )
@@ -146,8 +166,15 @@ def tile_list_sigm_mulP_kernel(
                 stop=True,
             )
 
-        x_quads = x_bf[:].rearrange("p (j t) -> p j t", t=SLOTS)
-        deal_bytes(wg_dealt[:], wg_raw[:], 2)
+        def x_cols(j0, j1):
+            part = int(j0 >= X_PARTS[1][0])
+            at = X_PARTS[part][0]
+            return x_bf[part][:, SLOTS * (j0 - at) : SLOTS * (j1 - at)]
+
+        def x_quads(j0, j1):
+            return x_cols(j0, j1).rearrange("p (j t) -> p j t", t=SLOTS)
+
+        deal_bytes(wg_dealt[:].bitcast(U16), wg_raw[:].bitcast(U16), 1)
         make_identity(nc, ident[:])
         warm = keep.tile([P, 1], F32, name="warm")
         nc.scalar.activation(warm[:], ident[:, 0:1], SIGMOID)
@@ -167,17 +194,29 @@ def tile_list_sigm_mulP_kernel(
             for at in range(j0, j1, C):
                 nc.tensor.transpose(spread[:, at - j0 : at - j0 + C], w_cols[:, at : at + C], ident[:])
             nc.scalar.copy(weight[:, j0:j1], spread[:])
+        nc.scalar.copy(weight_first[:], weight[:, :C])
 
         for j0, j1 in FIRST_PICKS[0]:
             gather(LOAD_ORDER[0], j0, j1)
         for j0, j1 in FIRST_PICKS[1]:
             gather(LOAD_ORDER[1], j0, j1)
         low_slots = picked[:, : 2 * J].rearrange("p (t j) -> p j t", t=2)
-        for j0, j1 in FIRST_PICKS[1]:
-            nc.scalar.copy(x_quads[:, j0:j1, 0:2], low_slots[:, j0:j1, :])
+        for j0, j1 in ((0, J // 2), (J // 2, 5 * C), (5 * C, J)):
+            nc.scalar.copy(x_quads(j0, j1)[:, :, 0:2], low_slots[:, j0:j1, :])
         for j0, j1 in FIRST_PICKS[2]:
             gather(LOAD_ORDER[2], j0, j1)
-        deal_bytes(w_sc[:], w_sc_raw[:], 1)
+
+        idle = psum3.tile([P, R], F32, name="ysum")
+        for m in range(2):
+            nc.tensor.matmul_mx(
+                out=idle[:],
+                lhsT=wd_raw[:, m * P : (m + 1) * P].bitcast(FP8X4),
+                lhsT_scale=w_sc_raw[WD_ROWS:, m * P : (m + 1) * P],
+                rhs=wd_raw[:].bitcast(FP8X4),
+                rhs_scale=w_sc_raw[WD_ROWS:, :],
+                start=True,
+                stop=True,
+            )
 
         sig = {}
         ub = {}
@@ -188,46 +227,55 @@ def tile_list_sigm_mulP_kernel(
             return slice(SLOTS * c * C, SLOTS * (c + 1) * C)
 
         def results(n):
-            return res[n][:].rearrange("p (t j) -> p t j", t=SLOTS)
+            return res[n].rearrange("p (t j) -> p t j", t=SLOTS)
 
         def g_of(n, u):
-            half, j0 = divmod(2 * n * C, J // 2)
-            return g_part[2 * half + u][:, :, j0 : j0 + 2 * C]
+            return g_part[n, u]
 
         def store(n, u):
             slots = slice(2 * u, 2 * u + 2)
             nc.sync.dma_start(out_rows[:, slots, 2 * n * C : 2 * (n + 1) * C], results(n)[:, slots, :])
 
+        def last_at(c):
+            if c < FREE:
+                return PICKS_AT[2] + c * C
+            if AFTER.get(c - 1) == AFTER[c]:
+                return last_at(AFTER[c])
+            return PICKS_AT[3] + AFTER[c] * C
+
         def pick(c):
-            gather(LOAD_ORDER[3], c * C, (c + 1) * C)
-            if c == 1:
-                deal_words(wu_dealt, wu_raw)
+            gather(LOAD_ORDER[3], c * C, (c + 1) * C, last_at(c))
 
         def round_x(c):
-            high_slots = picked[:, PICKS_AT[2] + c * C : PICKS_AT[2] + (c + 2 * AHEAD) * C]
+            high_slots = picked[:, last_at(c) : 2 * (PICKS_AT[3] + c * C) - last_at(c)]
             nc.scalar.copy(
-                x_quads[:, c * C : (c + 1) * C, 2:4],
+                x_quads(c * C, (c + 1) * C)[:, :, 2:4],
                 high_slots.rearrange("p (t x) -> p x t", t=2)[:, :C, :],
             )
 
-        def up(c):
-            quantize(x_codes, x_sc, x_bf[:, wide(c)], c, c + 1)
-            ga = psum2.tile([P, SLOTS, C], F32, name="ga")
-            ub[c] = psum3.tile([P, SLOTS, C], F32, name="ub")
-            cols = slice(c * C, (c + 1) * C)
+        ga = {}
+
+        def quant_x(c):
+            quantize(x_codes, x_sc, x_cols(c * C, (c + 1) * C), c, c + 1)
+
+        def up_gate(c):
+            ga[c] = psum2.tile([P, SLOTS, C], F32, name="ga")
             for t in range(SLOTS):
                 weights = wg_dealt[:, 2 * t * P : 2 * (t + 1) * P].bitcast(FP4X4)
-                product(ga[:, t, :], weights, WG_ROWS, t, x_codes, x_sc, cols)
+                product(ga[c][:, t, :], weights, WG_ROWS, t, x_codes, x_sc, slice(c * C, (c + 1) * C))
+
+        def up_value(c):
+            ub[c] = psum3.tile([P, SLOTS, C], F32, name="ub")
             for t in range(SLOTS):
                 weights = wu_dealt[:, t * P : (t + 1) * P].bitcast(FP8X4)
-                product(ub[c][:, t, :], weights, WU_ROWS, t, x_codes, x_sc, cols)
+                product(ub[c][:, t, :], weights, WU_ROWS, t, x_codes, x_sc, slice(c * C, (c + 1) * C))
+
+        def sigmoid(c):
             if c == CHUNKS - 2:
                 sig[c] = y_bf[:, : 2 * SLOTS * C].bitcast(F32).rearrange("p (j t) -> p j t", t=SLOTS)
             else:
                 sig[c] = ring.tile([P, C, SLOTS], F32, name="sig")
-            nc.scalar.activation(sig[c][:], ga[:].rearrange("p t j -> p j t"), SIGMOID)
-            if c == 1:
-                deal_words(wd_dealt, wd_raw)
+            nc.scalar.activation(sig[c][:], ga[c][:].rearrange("p t j -> p j t"), SIGMOID)
 
         def glu(c):
             nc.vector.tensor_tensor(
@@ -240,7 +288,7 @@ def tile_list_sigm_mulP_kernel(
         def down(n):
             quantize(h_codes, h_sc, h_bf[n], 2 * n, 2 * n + 2)
             cols = slice(2 * n * C, 2 * (n + 1) * C)
-            for u in range(2):
+            for u in (1, 0) if n < SIDE_PAIRS else (0, 1):
                 ysum[n, u] = psum3.tile([P, 2, 2 * C], F32, name="ysum")
                 for t in (2 * u, 2 * u + 1):
                     weights = wd_dealt[:, t * P : (t + 1) * P].bitcast(FP8X4)
@@ -256,21 +304,75 @@ def tile_list_sigm_mulP_kernel(
             nc.vector.tensor_tensor(results(n)[:, 2 * u : 2 * u + 2, :], ysum[n, u][:], g_of(n, u), MULT)
             store(n, u)
 
-        gates = {}
-        for n in range(PAIRS):
-            if n >= SIDE_PAIRS:
-                gates[DOWN_LAG + 2 * n + 2] = (n, 0)
-            gates[DOWN_LAG + 2 * n + (2 if n == 1 else 3)] = (n, 1)
-
-        for step in range(max(gates) + 1):
-            for stage, lag in ((pick, 0), (round_x, ROUND_LAG), (up, UP_LAG), (glu, GLU_LAG)):
-                if 0 <= step - lag < CHUNKS:
-                    stage(step - lag)
-            n, u = divmod(step - DOWN_LAG, 2)
-            if u == 1 and 0 <= n < PAIRS:
-                down(n)
-            if step in gates:
-                gate(*gates[step])
+        pick(0)
+        round_x(0)
+        pick(1)
+        round_x(1)
+        pick(2)
+        round_x(2)
+        pick(3)
+        round_x(3)
+        deal_bytes(w_sc[:], w_sc_raw[:], 1)
+        quant_x(0)
+        up_gate(0)
+        pick(4)
+        round_x(4)
+        quant_x(1)
+        up_gate(1)
+        deal_words(wu_dealt, wu_raw)
+        up_value(0)
+        up_value(1)
+        sigmoid(0)
+        sigmoid(1)
+        quant_x(2)
+        up_gate(2)
+        quant_x(3)
+        pick(7)
+        pick(5)
+        pick(6)
+        quant_x(4)
+        deal_words(wd_dealt, wd_raw, nc.gpsimd)
+        glu(0)
+        glu(1)
+        round_x(5)
+        up_gate(3)
+        up_value(2)
+        sigmoid(2)
+        round_x(6)
+        up_value(3)
+        sigmoid(3)
+        up_gate(4)
+        up_value(4)
+        quant_x(5)
+        round_x(7)
+        quant_x(6)
+        quant_x(7)
+        sigmoid(4)
+        down(0)
+        glu(2)
+        up_gate(5)
+        sigmoid(5)
+        glu(3)
+        up_value(5)
+        gate(0, 1)
+        down(1)
+        up_gate(6)
+        sigmoid(6)
+        glu(4)
+        up_value(6)
+        up_gate(7)
+        glu(5)
+        up_value(7)
+        sigmoid(7)
+        gate(1, 1)
+        down(2)
+        glu(6)
+        glu(7)
+        gate(2, 0)
+        down(3)
+        gate(2, 1)
+        gate(3, 0)
+        gate(3, 1)
 
         for n in range(PAIRS):
             last = n == PAIRS - 1

@@ -26,13 +26,15 @@ LANES = 16
 
 LOAD_ORDER = (0, 1, 3, 2)
 FIRST_PICKS = (((0, 128), (128, 384), (384, 768), (768, J)), ((0, J // 2), (J // 2, J)), ((0, J),))
-X_PARTS = ((0, 5 * C), (5 * C, J))
 FREE = 4
 PICKS_AT = (0, J, 2 * J, 2 * J + FREE * C)
-AFTER = {4: 0, 5: 4, 6: 4, 7: 3}
+LATE_AT = (PICKS_AT[3], PICKS_AT[3] + 4 * C, PICKS_AT[3], PICKS_AT[3] + 3 * C)
+PICKS_WIDTH = PICKS_AT[3] + 12 * C
+AHEAD = FREE + 1
+X_PARTS = ((0, AHEAD * C), (AHEAD * C, J))
 SCALE_LOADS = ((0, 4), (4, 9), (9, 12))
 WG_ROWS, WU_ROWS, WD_ROWS = 0, 4, 8
-ROUND_LAG, UP_LAG, GLU_LAG, DOWN_LAG = 1, 2, 4, 5
+UB_BANKS = 3
 SIDE_PAIRS = 2
 LAST_CUT = 80
 WORD_STORES = ((0, 4), (4, 6), (6, 8))
@@ -45,7 +47,7 @@ def tile_list_sigm_mulP_kernel(
     with ExitStack() as ctx:
         keep = ctx.enter_context(tc.tile_pool(name="keep", bufs=1))
         ring = ctx.enter_context(tc.tile_pool(name="ring", bufs=CHUNKS))
-        psum3 = ctx.enter_context(tc.psum_pool(name="psum3", bufs=3))
+        psum3 = ctx.enter_context(tc.psum_pool(name="psum3", bufs=UB_BANKS))
         psum2 = ctx.enter_context(tc.psum_pool(name="psum2", bufs=2))
 
         offsets = keep.tile([P, J // LANES], U16, name="offsets")
@@ -71,10 +73,8 @@ def tile_list_sigm_mulP_kernel(
             g_part[n, 0] = g_low[:, :, 2 * n * C : 2 * (n + 1) * C]
             for u in range(2):
                 g_part[2 + n, u] = g_late[:, 2 * u : 2 * u + 2, 2 * n * C : 2 * (n + 1) * C]
-        picked = keep.tile([P, 2 * J + 18 * C], F32, name="picked")
-        x_bf = [
-            keep.tile([P, SLOTS * (j1 - j0)], BF16, name=f"x_bf{j0}", align_bytes=64) for j0, j1 in X_PARTS
-        ]
+        picked = keep.tile([P, PICKS_WIDTH], F32, name="picked")
+        x_bf = [keep.tile([P, SLOTS * (j1 - j0)], BF16, name=f"x_bf{j0}", align_bytes=64) for j0, j1 in X_PARTS]
         res = [
             g_then_res[:, 4 * C :] if n == 1 else keep.tile([P, 2 * SLOTS * C], F32, name=f"res{n}", align_bytes=64)[:]
             for n in range(PAIRS)
@@ -127,22 +127,20 @@ def tile_list_sigm_mulP_kernel(
         nc.sync.dma_start(g_part[1, 1], g_rows[:, 2:4, 2 * C : 4 * C])
         nc.sync.dma_start(g_late[:], g_rows[:, :, 4 * C :])
 
-        def gather(t, j0, j1, at=None):
-            at = PICKS_AT[t] + j0 if at is None else at
+        def gather(t, j0, j1, at, factor):
             nc.vector.tensor_tensor(
                 picked[:, at : at + j1 - j0],
                 x_slot[t][:].indirect(offsets[:, j0 // LANES : j1 // LANES]),
-                weight_first[:] if (t, j0) == (LOAD_ORDER[3], 0) else weight[:, j0:j1],
+                factor,
                 MULT,
             )
 
-        def deal_bytes(dst, src, width):
+        def deal_narrow(dst, src):
             nc.vector.tensor_copy(
-                dst.rearrange("p (t m b) -> p t m b", t=SLOTS, b=width),
-                src.rearrange("p (m t b) -> p t m b", t=SLOTS, b=width),
+                dst.rearrange("p (t m) -> p t m", t=SLOTS), src.rearrange("p (m t) -> p t m", t=SLOTS)
             )
 
-        def deal_words(dst, src, engine=nc.vector):
+        def deal_words(engine, dst, src):
             engine.tensor_copy(
                 dst[:].bitcast(I32).rearrange("p (t m i) -> p m t i", t=SLOTS, i=4),
                 src[:].bitcast(I32).rearrange("p (m i t) -> p m t i", t=SLOTS, i=4),
@@ -174,7 +172,7 @@ def tile_list_sigm_mulP_kernel(
         def x_quads(j0, j1):
             return x_cols(j0, j1).rearrange("p (j t) -> p j t", t=SLOTS)
 
-        deal_bytes(wg_dealt[:].bitcast(U16), wg_raw[:].bitcast(U16), 1)
+        deal_narrow(wg_dealt[:].bitcast(U16), wg_raw[:].bitcast(U16))
         make_identity(nc, ident[:])
         warm = keep.tile([P, 1], F32, name="warm")
         nc.scalar.activation(warm[:], ident[:, 0:1], SIGMOID)
@@ -197,14 +195,14 @@ def tile_list_sigm_mulP_kernel(
         nc.scalar.copy(weight_first[:], weight[:, :C])
 
         for j0, j1 in FIRST_PICKS[0]:
-            gather(LOAD_ORDER[0], j0, j1)
+            gather(LOAD_ORDER[0], j0, j1, PICKS_AT[LOAD_ORDER[0]] + j0, weight[:, j0:j1])
         for j0, j1 in FIRST_PICKS[1]:
-            gather(LOAD_ORDER[1], j0, j1)
+            gather(LOAD_ORDER[1], j0, j1, PICKS_AT[LOAD_ORDER[1]] + j0, weight[:, j0:j1])
         low_slots = picked[:, : 2 * J].rearrange("p (t j) -> p j t", t=2)
-        for j0, j1 in ((0, J // 2), (J // 2, 5 * C), (5 * C, J)):
+        for j0, j1 in ((0, J // 2), (J // 2, AHEAD * C), (AHEAD * C, J)):
             nc.scalar.copy(x_quads(j0, j1)[:, :, 0:2], low_slots[:, j0:j1, :])
         for j0, j1 in FIRST_PICKS[2]:
-            gather(LOAD_ORDER[2], j0, j1)
+            gather(LOAD_ORDER[2], j0, j1, PICKS_AT[LOAD_ORDER[2]] + j0, weight[:, j0:j1])
 
         idle = psum3.tile([P, R], F32, name="ysum")
         for m in range(2):
@@ -218,6 +216,7 @@ def tile_list_sigm_mulP_kernel(
                 stop=True,
             )
 
+        ga = {}
         sig = {}
         ub = {}
         ysum = {}
@@ -229,22 +228,16 @@ def tile_list_sigm_mulP_kernel(
         def results(n):
             return res[n].rearrange("p (t j) -> p t j", t=SLOTS)
 
-        def g_of(n, u):
-            return g_part[n, u]
-
         def store(n, u):
             slots = slice(2 * u, 2 * u + 2)
             nc.sync.dma_start(out_rows[:, slots, 2 * n * C : 2 * (n + 1) * C], results(n)[:, slots, :])
 
         def last_at(c):
-            if c < FREE:
-                return PICKS_AT[2] + c * C
-            if AFTER.get(c - 1) == AFTER[c]:
-                return last_at(AFTER[c])
-            return PICKS_AT[3] + AFTER[c] * C
+            return PICKS_AT[2] + c * C if c < FREE else LATE_AT[c - FREE]
 
         def pick(c):
-            gather(LOAD_ORDER[3], c * C, (c + 1) * C, last_at(c))
+            factor = weight[:, c * C : (c + 1) * C] if c else weight_first[:]
+            gather(LOAD_ORDER[3], c * C, (c + 1) * C, last_at(c), factor)
 
         def round_x(c):
             high_slots = picked[:, last_at(c) : 2 * (PICKS_AT[3] + c * C) - last_at(c)]
@@ -252,8 +245,6 @@ def tile_list_sigm_mulP_kernel(
                 x_quads(c * C, (c + 1) * C)[:, :, 2:4],
                 high_slots.rearrange("p (t x) -> p x t", t=2)[:, :C, :],
             )
-
-        ga = {}
 
         def quant_x(c):
             quantize(x_codes, x_sc, x_cols(c * C, (c + 1) * C), c, c + 1)
@@ -277,6 +268,11 @@ def tile_list_sigm_mulP_kernel(
                 sig[c] = ring.tile([P, C, SLOTS], F32, name="sig")
             nc.scalar.activation(sig[c][:], ga[c][:].rearrange("p t j -> p j t"), SIGMOID)
 
+        def up(c):
+            up_gate(c)
+            up_value(c)
+            sigmoid(c)
+
         def glu(c):
             nc.vector.tensor_tensor(
                 h_bf[c // 2][:, wide(c % 2)].rearrange("p (j t) -> p j t", t=SLOTS),
@@ -294,85 +290,57 @@ def tile_list_sigm_mulP_kernel(
                     weights = wd_dealt[:, t * P : (t + 1) * P].bitcast(FP8X4)
                     product(ysum[n, u][:, t % 2, :], weights, WD_ROWS, t, h_codes, h_sc, cols)
             if 1 <= n <= SIDE_PAIRS:
-                nc.gpsimd.tensor_tensor(results(n - 1)[:, 0:2, :], y_copy[n - 1][:], g_of(n - 1, 0), MULT)
+                nc.gpsimd.tensor_tensor(results(n - 1)[:, 0:2, :], y_copy[n - 1][:], g_part[n - 1, 0], MULT)
                 store(n - 1, 0)
             if n < SIDE_PAIRS:
                 y_copy[n] = keep.tile([P, 2, 2 * C], F32, name=f"y_copy{n}")
                 nc.scalar.copy(y_copy[n][:], ysum[n, 0][:])
 
         def gate(n, u):
-            nc.vector.tensor_tensor(results(n)[:, 2 * u : 2 * u + 2, :], ysum[n, u][:], g_of(n, u), MULT)
+            nc.vector.tensor_tensor(results(n)[:, 2 * u : 2 * u + 2, :], ysum[n, u][:], g_part[n, u], MULT)
             store(n, u)
 
-        pick(0)
-        round_x(0)
-        pick(1)
-        round_x(1)
-        pick(2)
-        round_x(2)
-        pick(3)
-        round_x(3)
-        deal_bytes(w_sc[:], w_sc_raw[:], 1)
+        for c in range(FREE):
+            pick(c)
+            round_x(c)
+        deal_narrow(w_sc[:], w_sc_raw[:])
         quant_x(0)
         up_gate(0)
-        pick(4)
-        round_x(4)
+        pick(FREE)
+        round_x(FREE)
         quant_x(1)
         up_gate(1)
-        deal_words(wu_dealt, wu_raw)
-        up_value(0)
-        up_value(1)
-        sigmoid(0)
-        sigmoid(1)
-        quant_x(2)
-        up_gate(2)
-        quant_x(3)
-        pick(7)
-        pick(5)
-        pick(6)
-        quant_x(4)
-        deal_words(wd_dealt, wd_raw, nc.gpsimd)
+        deal_words(nc.vector, wu_dealt, wu_raw)
+        for stage in (up_value, sigmoid):
+            stage(0)
+            stage(1)
+        for c in range(2, FREE):
+            quant_x(c)
+        for c in (7, 5, 6):
+            pick(c)
+        quant_x(FREE)
+        deal_words(nc.gpsimd, wd_dealt, wd_raw)
         glu(0)
         glu(1)
-        round_x(5)
-        up_gate(3)
-        up_value(2)
-        sigmoid(2)
-        round_x(6)
-        up_value(3)
-        sigmoid(3)
-        up_gate(4)
-        up_value(4)
-        quant_x(5)
-        round_x(7)
-        quant_x(6)
-        quant_x(7)
-        sigmoid(4)
+
+        for c in range(AHEAD, CHUNKS):
+            round_x(c)
+            up(c - UB_BANKS)
+        for c in range(AHEAD, CHUNKS):
+            quant_x(c)
         down(0)
-        glu(2)
-        up_gate(5)
-        sigmoid(5)
-        glu(3)
-        up_value(5)
-        gate(0, 1)
-        down(1)
-        up_gate(6)
-        sigmoid(6)
-        glu(4)
-        up_value(6)
-        up_gate(7)
-        glu(5)
-        up_value(7)
-        sigmoid(7)
-        gate(1, 1)
-        down(2)
-        glu(6)
-        glu(7)
-        gate(2, 0)
-        down(3)
-        gate(2, 1)
-        gate(3, 0)
-        gate(3, 1)
+
+        for c in range(2, CHUNKS):
+            glu(c)
+            if c + UB_BANKS < CHUNKS:
+                up(c + UB_BANKS)
+            if c % 2:
+                n = c // 2
+                gate(n - 1, 1 if n - 1 < SIDE_PAIRS else 0)
+                down(n)
+        gate(PAIRS - 2, 1)
+        for u in range(2):
+            gate(PAIRS - 1, u)
 
         for n in range(PAIRS):
             last = n == PAIRS - 1

@@ -24,15 +24,10 @@ CHUNKS = J // C
 PAIRS = CHUNKS // 2
 LANES = 16
 
-LOAD_ORDER = (0, 1, 3, 2)
-FIRST_PICKS = (((0, 128), (128, 384), (384, 768), (768, J)), ((0, J // 2), (J // 2, J)), ((0, J),))
-FREE = 4
-PICKS_AT = (0, J, 2 * J, 2 * J + FREE * C)
-LATE_AT = (PICKS_AT[3], PICKS_AT[3] + 4 * C, PICKS_AT[3], PICKS_AT[3] + 3 * C)
-PICKS_WIDTH = PICKS_AT[3] + 12 * C
-AHEAD = FREE + 1
-X_PARTS = ((0, AHEAD * C), (AHEAD * C, J))
-SCALE_LOADS = ((0, 4), (4, 9), (9, 12))
+SPREAD = ((0, C), (C, 3 * C), (3 * C, 6 * C), (6 * C, J))
+SECOND_CUT = 3 * C
+FRONT = 5
+SIDE_LOADS = 8
 WG_ROWS, WU_ROWS, WD_ROWS = 0, 4, 8
 UB_BANKS = 3
 SIDE_PAIRS = 2
@@ -50,21 +45,41 @@ def tile_list_sigm_mulP_kernel(
         psum3 = ctx.enter_context(tc.psum_pool(name="psum3", bufs=UB_BANKS))
         psum2 = ctx.enter_context(tc.psum_pool(name="psum2", bufs=2))
 
+        def sbuf(name, shape, dtype, on=None):
+            return keep.tile([P] + shape, dtype, name=name, tag=on or name, align_bytes=64)
+
         offsets = keep.tile([P, J // LANES], U16, name="offsets")
-        weight = keep.tile([P, J], F32, name="weight")
-        x_slot = [keep.tile([P, T], F32, name=f"x_slot{t}") for t in range(SLOTS)]
-        wg_raw = keep.tile([P, 2 * R], U8, name="wg_raw", align_bytes=64)
-        wu_raw = keep.tile([P, R], U32, name="wu_raw", align_bytes=64)
-        wd_raw = keep.tile([P, N], U32, name="wd_raw", align_bytes=64)
-        w_sc_raw = keep.tile([P, R], U8, name="w_sc_raw", align_bytes=64)
-        wg_dealt = keep.tile([P, 2 * R], U8, name="wg_dealt", align_bytes=64)
-        wu_dealt = keep.tile([P, R], U32, name="wu_dealt", align_bytes=64)
-        weight_first = keep.tile([P, C], F32, name="weight_first", align_bytes=64)
-        w_sc = keep.tile([P, R], U8, name="w_sc", tag="weight_first", align_bytes=64)
-        g_low = keep.tile([P, 2, 4 * C], F32, name="g_low", align_bytes=64)
-        g_then_res = keep.tile([P, 6 * 2 * C], F32, name="g_then_res", align_bytes=64)
-        g_second = keep.tile([P, 2 * 2 * C], F32, name="g_second", align_bytes=64)
-        g_late = keep.tile([P, SLOTS, 4 * C], F32, name="g_late", align_bytes=64)
+        ident = sbuf("ident", [P], F32)
+        w_rows = sbuf("w_rows", [C], F32)
+        w_cols = sbuf("w_cols", [J], F32)
+        weight = sbuf("weight", [J], F32)
+        x_slot = [sbuf(f"x_slot{t}", [T], F32) for t in range(SLOTS)]
+        wg_raw = sbuf("wg_raw", [2 * R], U8)
+        wu_raw = sbuf("wu_raw", [R], U32)
+        wd_raw = sbuf("wd_raw", [N], U32)
+        w_sc_raw = sbuf("w_sc_raw", [R], U8)
+        w_sc = sbuf("w_sc", [R], U8)
+        wg_dealt = sbuf("wg_dealt", [2 * R], U8)
+
+        low_picks = sbuf("low_picks", [2 * J], F32)
+        front = sbuf("front", [(2 * FRONT - 1) * C], F32, on="w_sc_raw")
+        back = sbuf("back", [(4 + CHUNKS - FRONT) * C], F32)
+        x_first = sbuf("x_first", [SLOTS * C], BF16)
+        x_mid = sbuf("x_mid", [2 * SLOTS * C], BF16)
+        x_last = sbuf("x_last", [(CHUNKS - FRONT) * SLOTS * C], BF16)
+        x_parts = (
+            (0, 1, x_first[:]),
+            (1, 3, back[:, : 4 * C].bitcast(BF16)),
+            (3, FRONT, x_mid[:]),
+            (FRONT, CHUNKS, x_last[:]),
+        )
+        wu_dealt = sbuf("wu_dealt", [R], U32, on="x_first")
+        wd_dealt = sbuf("wd_dealt", [N], U32, on="x_mid")
+
+        g_low = sbuf("g_low", [2, 4 * C], F32)
+        g_then_res = sbuf("g_then_res", [6 * 2 * C], F32)
+        g_second = sbuf("g_second", [2 * 2 * C], F32)
+        g_late = sbuf("g_late", [SLOTS, 4 * C], F32)
         g_part = {
             (0, 1): g_then_res[:, : 4 * C].rearrange("p (t j) -> p t j", t=2),
             (1, 1): g_second[:].rearrange("p (t j) -> p t j", t=2),
@@ -73,72 +88,60 @@ def tile_list_sigm_mulP_kernel(
             g_part[n, 0] = g_low[:, :, 2 * n * C : 2 * (n + 1) * C]
             for u in range(2):
                 g_part[2 + n, u] = g_late[:, 2 * u : 2 * u + 2, 2 * n * C : 2 * (n + 1) * C]
-        picked = keep.tile([P, PICKS_WIDTH], F32, name="picked")
-        x_bf = [keep.tile([P, SLOTS * (j1 - j0)], BF16, name=f"x_bf{j0}", align_bytes=64) for j0, j1 in X_PARTS]
         res = [
-            g_then_res[:, 4 * C :] if n == 1 else keep.tile([P, 2 * SLOTS * C], F32, name=f"res{n}", align_bytes=64)[:]
-            for n in range(PAIRS)
+            g_then_res[:, 4 * C :] if n == 1 else sbuf(f"res{n}", [2 * SLOTS * C], F32)[:] for n in range(PAIRS)
         ]
-        wd_dealt = keep.tile([P, N], U32, name="wd_dealt", tag="x_bf0", align_bytes=64)
-        h_first = keep.tile([P, 2 * SLOTS * C], BF16, name="h_first", align_bytes=64)
+        h_first = sbuf("h_first", [2 * SLOTS * C], BF16)
         h_bf = [
             h_first[:],
             res[0][:, : 4 * C].bitcast(BF16),
             g_then_res[:, 2 * C : 6 * C].bitcast(BF16),
             g_second[:].bitcast(BF16),
         ]
-        y_bf = keep.tile([P, SLOTS * J], BF16, name="y_bf", align_bytes=64)
-        x_codes = keep.tile([P, J], U32, name="x_codes", align_bytes=64)
-        h_codes = keep.tile([P, J], U32, name="h_codes", align_bytes=64)
-        y_codes = keep.tile([P, J], U32, name="y_codes", align_bytes=64)
-        x_sc = keep.tile([P, J], U8, name="x_sc", align_bytes=64)
-        h_sc = keep.tile([P, J], U8, name="h_sc", align_bytes=64)
-        y_sc = keep.tile([P, J], U8, name="y_sc", align_bytes=64)
-
-        ident = keep.tile([P, P], F32, name="ident")
-        w_rows = keep.tile([P, C], F32, name="w_rows")
-        w_cols = keep.tile([P, J], F32, name="w_cols")
+        y_bf = sbuf("y_bf", [SLOTS * J], BF16)
+        x_codes, h_codes, y_codes = [sbuf(f"{a}_codes", [J], U32) for a in "xhy"]
+        x_sc, h_sc, y_sc = [sbuf(f"{a}_sc", [J], U8) for a in "xhy"]
 
         x_rows = xT.rearrange("(p t) i -> p t i", t=SLOTS)
         g_rows = g.rearrange("(p t) j -> p t j", t=SLOTS)
         out_rows = out_0.rearrange("(p t) j -> p t j", t=SLOTS)
         out_words = out_1[0].rearrange("p j t -> p (j t)").bitcast(I32)
 
-        def load_scale_rows(first, last):
+        def load_scale_rows(queue, first, last):
             for n in range(first, last):
                 a, q = divmod(n, 4)
-                nc.sync.dma_start(
+                queue.dma_start(
                     w_sc_raw[32 * q + 4 * a : 32 * q + 4 * a + 4, :].bitcast(I32),
                     (wg_scales, wu_scales, wd_scales)[a][0, 4 * q : 4 * q + 4, :].bitcast(I32),
                 )
 
+        def load_words(dst, words):
+            nc.sync.dma_start(dst[:].bitcast(I32), words[0].rearrange("p n t -> p (n t)").bitcast(I32))
+
         nc.vector.memset(w_sc_raw[:].bitcast(I32), 0)
+        make_identity(nc, ident[:])
+        load_scale_rows(nc.gpsimd, 0, SIDE_LOADS)
         nc.sync.dma_start(w_rows[:], wgt[0:P:8, :].rearrange("a (c x) -> a c x", x=C))
         nc.sync.dma_start(offsets[:], offs)
-        nc.sync.dma_start(wg_raw[:].bitcast(I32), wg_words[0].bitcast(I32))
-        for n, t in enumerate(LOAD_ORDER):
+        for t in (0, 1, 3):
             nc.sync.dma_start(x_slot[t][:], x_rows[:, t, :])
-            if n < len(SCALE_LOADS):
-                load_scale_rows(*SCALE_LOADS[n])
-        nc.sync.dma_start(wd_raw[:].bitcast(I32), wd_words[0].rearrange("p n t -> p (n t)").bitcast(I32))
-        nc.sync.dma_start(wu_raw[:].bitcast(I32), wu_words[0].rearrange("p r t -> p (r t)").bitcast(I32))
+        load_scale_rows(nc.sync, SIDE_LOADS, 12)
+        nc.sync.dma_start(wg_raw[:].bitcast(I32), wg_words[0].bitcast(I32))
+        nc.sync.dma_start(x_slot[2][:], x_rows[:, 2, :])
+        load_words(wu_raw, wu_words)
+        load_words(wd_raw, wd_words)
         nc.sync.dma_start(g_part[0, 1], g_rows[:, 2:4, : 2 * C])
         nc.sync.dma_start(g_low[:], g_rows[:, 0:2, : 4 * C])
         nc.sync.dma_start(g_part[1, 1], g_rows[:, 2:4, 2 * C : 4 * C])
         nc.sync.dma_start(g_late[:], g_rows[:, :, 4 * C :])
 
-        def gather(t, j0, j1, at, factor):
+        def gather(dst, t, j0, j1):
             nc.vector.tensor_tensor(
-                picked[:, at : at + j1 - j0],
-                x_slot[t][:].indirect(offsets[:, j0 // LANES : j1 // LANES]),
-                factor,
-                MULT,
+                dst, x_slot[t][:].indirect(offsets[:, j0 // LANES : j1 // LANES]), weight[:, j0:j1], MULT
             )
 
-        def deal_narrow(dst, src):
-            nc.vector.tensor_copy(
-                dst.rearrange("p (t m) -> p t m", t=SLOTS), src.rearrange("p (m t) -> p t m", t=SLOTS)
-            )
+        def deal_narrow(copy, dst, src):
+            copy(dst.rearrange("p (t m) -> p t m", t=SLOTS), src.rearrange("p (m t) -> p t m", t=SLOTS))
 
         def deal_words(engine, dst, src):
             engine.tensor_copy(
@@ -164,21 +167,20 @@ def tile_list_sigm_mulP_kernel(
                 stop=True,
             )
 
-        def x_cols(j0, j1):
-            part = int(j0 >= X_PARTS[1][0])
-            at = X_PARTS[part][0]
-            return x_bf[part][:, SLOTS * (j0 - at) : SLOTS * (j1 - at)]
+        def wide(c):
+            return slice(SLOTS * c * C, SLOTS * (c + 1) * C)
 
-        def x_quads(j0, j1):
-            return x_cols(j0, j1).rearrange("p (j t) -> p j t", t=SLOTS)
+        def x_chunk(c):
+            first, held = [(c0, part) for c0, c1, part in x_parts if c0 <= c < c1][0]
+            return held[:, wide(c - first)]
 
-        deal_narrow(wg_dealt[:].bitcast(U16), wg_raw[:].bitcast(U16))
-        make_identity(nc, ident[:])
-        warm = keep.tile([P, 1], F32, name="warm")
+        def quads(ap):
+            return ap.rearrange("p (j t) -> p j t", t=SLOTS)
+
+        warm = sbuf("warm", [1], F32)
         nc.scalar.activation(warm[:], ident[:, 0:1], SIGMOID)
 
-        pieces = FIRST_PICKS[0]
-        for copy, share in ((nc.scalar.copy, pieces[:2]), (nc.vector.tensor_copy, pieces[2:])):
+        for copy, share in ((nc.scalar.copy, SPREAD[:1]), (nc.vector.tensor_copy, SPREAD[1:])):
             turned = psum3.tile([P, P], F32, name="ysum")
             nc.tensor.transpose(turned[:], w_rows[:], ident[:])
             by_chunk = turned[:].rearrange("x (a c) -> x c a", c=CHUNKS)
@@ -187,31 +189,32 @@ def tile_list_sigm_mulP_kernel(
                     w_cols[:, j0:j1].rearrange("x (c a r) -> x c a r", a=16, r=8),
                     by_chunk[:, j0 // C : j1 // C, :].unsqueeze(3).broadcast_to([P, (j1 - j0) // C, 16, 8]),
                 )
-        for j0, j1 in pieces:
+        for j0, j1 in SPREAD:
             spread = psum3.tile([P, j1 - j0], F32, name="ub")
             for at in range(j0, j1, C):
                 nc.tensor.transpose(spread[:, at - j0 : at - j0 + C], w_cols[:, at : at + C], ident[:])
             nc.scalar.copy(weight[:, j0:j1], spread[:])
-        nc.scalar.copy(weight_first[:], weight[:, :C])
 
-        for j0, j1 in FIRST_PICKS[0]:
-            gather(LOAD_ORDER[0], j0, j1, PICKS_AT[LOAD_ORDER[0]] + j0, weight[:, j0:j1])
-        for j0, j1 in FIRST_PICKS[1]:
-            gather(LOAD_ORDER[1], j0, j1, PICKS_AT[LOAD_ORDER[1]] + j0, weight[:, j0:j1])
-        low_slots = picked[:, : 2 * J].rearrange("p (t j) -> p j t", t=2)
-        for j0, j1 in ((0, J // 2), (J // 2, AHEAD * C), (AHEAD * C, J)):
-            nc.scalar.copy(x_quads(j0, j1)[:, :, 0:2], low_slots[:, j0:j1, :])
-        for j0, j1 in FIRST_PICKS[2]:
-            gather(LOAD_ORDER[2], j0, j1, PICKS_AT[LOAD_ORDER[2]] + j0, weight[:, j0:j1])
+        for j0, j1 in SPREAD:
+            gather(low_picks[:, j0:j1], 0, j0, j1)
+        for j0, j1 in ((0, SECOND_CUT), (SECOND_CUT, J)):
+            gather(low_picks[:, J + j0 : J + j1], 1, j0, j1)
+        low_slots = low_picks[:].rearrange("p (t j) -> p j t", t=2)
+        for c0, c1, part in x_parts:
+            nc.scalar.copy(quads(part)[:, :, 0:2], low_slots[:, c0 * C : c1 * C, :])
+        deal_narrow(nc.scalar.copy, wg_dealt[:].bitcast(U16), wg_raw[:].bitcast(U16))
+        gather(back[:, 4 * C :], 3, FRONT * C, J)
+        deal_narrow(nc.vector.tensor_copy, w_sc[:], w_sc_raw[:])
+        gather(front[:, (FRONT - 1) * C :], 3, 0, FRONT * C)
 
         idle = psum3.tile([P, R], F32, name="ysum")
         for m in range(2):
             nc.tensor.matmul_mx(
                 out=idle[:],
-                lhsT=wd_raw[:, m * P : (m + 1) * P].bitcast(FP8X4),
-                lhsT_scale=w_sc_raw[WD_ROWS:, m * P : (m + 1) * P],
-                rhs=wd_raw[:].bitcast(FP8X4),
-                rhs_scale=w_sc_raw[WD_ROWS:, :],
+                lhsT=wu_raw[:, m * P : (m + 1) * P].bitcast(FP8X4),
+                lhsT_scale=w_sc[WU_ROWS:, m * P : (m + 1) * P],
+                rhs=wu_raw[:].bitcast(FP8X4),
+                rhs_scale=w_sc[WU_ROWS:, :],
                 start=True,
                 stop=True,
             )
@@ -222,9 +225,6 @@ def tile_list_sigm_mulP_kernel(
         ysum = {}
         y_copy = {}
 
-        def wide(c):
-            return slice(SLOTS * c * C, SLOTS * (c + 1) * C)
-
         def results(n):
             return res[n].rearrange("p (t j) -> p t j", t=SLOTS)
 
@@ -232,22 +232,23 @@ def tile_list_sigm_mulP_kernel(
             slots = slice(2 * u, 2 * u + 2)
             nc.sync.dma_start(out_rows[:, slots, 2 * n * C : 2 * (n + 1) * C], results(n)[:, slots, :])
 
-        def last_at(c):
-            return PICKS_AT[2] + c * C if c < FREE else LATE_AT[c - FREE]
+        def high_blocks(c):
+            if c < FRONT:
+                return front[:].rearrange("p (b x) -> p b x", x=C), c, FRONT - 1 + c
+            return back[:].rearrange("p (b x) -> p b x", x=C), c - FRONT, 4 + c - FRONT
 
         def pick(c):
-            factor = weight[:, c * C : (c + 1) * C] if c else weight_first[:]
-            gather(LOAD_ORDER[3], c * C, (c + 1) * C, last_at(c), factor)
+            blocks, at = high_blocks(c)[:2]
+            gather(blocks[:, at, :], 2, c * C, (c + 1) * C)
 
         def round_x(c):
-            high_slots = picked[:, last_at(c) : 2 * (PICKS_AT[3] + c * C) - last_at(c)]
+            blocks, at, other = high_blocks(c)
             nc.scalar.copy(
-                x_quads(c * C, (c + 1) * C)[:, :, 2:4],
-                high_slots.rearrange("p (t x) -> p x t", t=2)[:, :C, :],
+                quads(x_chunk(c))[:, :, 2:4], blocks[:, at : other + 1 : other - at, :].rearrange("p t x -> p x t")
             )
 
         def quant_x(c):
-            quantize(x_codes, x_sc, x_cols(c * C, (c + 1) * C), c, c + 1)
+            quantize(x_codes, x_sc, x_chunk(c), c, c + 1)
 
         def up_gate(c):
             ga[c] = psum2.tile([P, SLOTS, C], F32, name="ga")
@@ -263,10 +264,10 @@ def tile_list_sigm_mulP_kernel(
 
         def sigmoid(c):
             if c == CHUNKS - 2:
-                sig[c] = y_bf[:, : 2 * SLOTS * C].bitcast(F32).rearrange("p (j t) -> p j t", t=SLOTS)
+                sig[c] = quads(y_bf[:, : 2 * SLOTS * C].bitcast(F32))
             else:
-                sig[c] = ring.tile([P, C, SLOTS], F32, name="sig")
-            nc.scalar.activation(sig[c][:], ga[c][:].rearrange("p t j -> p j t"), SIGMOID)
+                sig[c] = ring.tile([P, C, SLOTS], F32, name="sig")[:]
+            nc.scalar.activation(sig[c], ga[c][:].rearrange("p t j -> p j t"), SIGMOID)
 
         def up(c):
             up_gate(c)
@@ -275,10 +276,7 @@ def tile_list_sigm_mulP_kernel(
 
         def glu(c):
             nc.vector.tensor_tensor(
-                h_bf[c // 2][:, wide(c % 2)].rearrange("p (j t) -> p j t", t=SLOTS),
-                ub[c][:].rearrange("p t j -> p j t"),
-                sig[c][:],
-                MULT,
+                quads(h_bf[c // 2][:, wide(c % 2)]), ub[c][:].rearrange("p t j -> p j t"), sig[c], MULT
             )
 
         def down(n):
@@ -293,40 +291,40 @@ def tile_list_sigm_mulP_kernel(
                 nc.gpsimd.tensor_tensor(results(n - 1)[:, 0:2, :], y_copy[n - 1][:], g_part[n - 1, 0], MULT)
                 store(n - 1, 0)
             if n < SIDE_PAIRS:
-                y_copy[n] = keep.tile([P, 2, 2 * C], F32, name=f"y_copy{n}")
+                y_copy[n] = sbuf(f"y_copy{n}", [2, 2 * C], F32)
                 nc.scalar.copy(y_copy[n][:], ysum[n, 0][:])
 
         def gate(n, u):
             nc.vector.tensor_tensor(results(n)[:, 2 * u : 2 * u + 2, :], ysum[n, u][:], g_part[n, u], MULT)
             store(n, u)
 
-        for c in range(FREE):
+        for c in range(FRONT - 1):
             pick(c)
             round_x(c)
-        deal_narrow(w_sc[:], w_sc_raw[:])
         quant_x(0)
         up_gate(0)
-        pick(FREE)
-        round_x(FREE)
+        pick(FRONT - 1)
+        round_x(FRONT - 1)
         quant_x(1)
         up_gate(1)
         deal_words(nc.vector, wu_dealt, wu_raw)
         for stage in (up_value, sigmoid):
             stage(0)
             stage(1)
-        for c in range(2, FREE):
-            quant_x(c)
-        for c in (7, 5, 6):
-            pick(c)
-        quant_x(FREE)
+        pick(5)
+        pick(6)
+        quant_x(2)
+        quant_x(3)
+        pick(7)
+        quant_x(4)
         deal_words(nc.gpsimd, wd_dealt, wd_raw)
         glu(0)
         glu(1)
 
-        for c in range(AHEAD, CHUNKS):
+        for c in range(FRONT, CHUNKS):
             round_x(c)
             up(c - UB_BANKS)
-        for c in range(AHEAD, CHUNKS):
+        for c in range(FRONT, CHUNKS):
             quant_x(c)
         down(0)
 

@@ -25,9 +25,10 @@ PAIRS = CHUNKS // 2
 LANES = 16
 
 SPREAD = ((0, C), (C, 3 * C), (3 * C, 6 * C), (6 * C, J))
-SECOND_CUT = 3 * C
-FRONT = 5
-SIDE_LOADS = 8
+FREE = 4
+LATE_BLOCK = {4: FREE, 5: FREE + 4, 6: FREE, 7: FREE + 3}
+AHEAD = FREE + 1
+SCALE_LOADS = ((0, 5), (5, 9), (9, 12))
 WG_ROWS, WU_ROWS, WD_ROWS = 0, 4, 8
 UB_BANKS = 3
 SIDE_PAIRS = 2
@@ -62,43 +63,30 @@ def tile_list_sigm_mulP_kernel(
         wg_dealt = sbuf("wg_dealt", [2 * R], U8)
 
         low_picks = sbuf("low_picks", [2 * J], F32)
-        front = sbuf("front", [(2 * FRONT - 1) * C], F32, on="w_sc_raw")
-        back = sbuf("back", [(4 + CHUNKS - FRONT) * C], F32)
-        x_first = sbuf("x_first", [SLOTS * C], BF16)
-        x_mid = sbuf("x_mid", [2 * SLOTS * C], BF16)
-        x_last = sbuf("x_last", [(CHUNKS - FRONT) * SLOTS * C], BF16)
-        x_parts = (
-            (0, 1, x_first[:]),
-            (1, 3, back[:, : 4 * C].bitcast(BF16)),
-            (3, FRONT, x_mid[:]),
-            (FRONT, CHUNKS, x_last[:]),
-        )
+        high_picks = sbuf("high_picks", [(FREE + CHUNKS) * C], F32)
+        blocks = high_picks[:].rearrange("p (b x) -> p b x", x=C)
+        x_parts = [
+            (c0, c1, sbuf(name, [(c1 - c0) * SLOTS * C], BF16)[:])
+            for c0, c1, name in ((0, 1, "x_first"), (1, AHEAD, "x_mid"), (AHEAD, CHUNKS, "x_last"))
+        ]
         wu_dealt = sbuf("wu_dealt", [R], U32, on="x_first")
-        wd_dealt = sbuf("wd_dealt", [N], U32, on="x_mid")
+        wd_dealt = sbuf("wd_dealt", [N], U32, on="weight")
 
         g_low = sbuf("g_low", [2, 4 * C], F32)
-        g_then_res = sbuf("g_then_res", [6 * 2 * C], F32)
-        g_second = sbuf("g_second", [2 * 2 * C], F32)
         g_late = sbuf("g_late", [SLOTS, 4 * C], F32)
-        g_part = {
-            (0, 1): g_then_res[:, : 4 * C].rearrange("p (t j) -> p t j", t=2),
-            (1, 1): g_second[:].rearrange("p (t j) -> p t j", t=2),
-        }
-        for n in range(2):
+        g_part = {}
+        res = {}
+        h_bf = {n: sbuf(f"h_bf{n}", [2 * SLOTS * C], BF16)[:] for n in range(PAIRS - SIDE_PAIRS)}
+        for n in range(SIDE_PAIRS):
+            shared = sbuf(f"shared{n}", [12 * C], F32)
+            h_bf[n + 2] = shared[:, : 4 * C].bitcast(BF16)
+            res[n] = shared[:, 4 * C :]
+            g_part[n, 1] = shared[:, 3 * C // 2 : 11 * C // 2].rearrange("p (t j) -> p t j", t=2)
             g_part[n, 0] = g_low[:, :, 2 * n * C : 2 * (n + 1) * C]
+            res[n + 2] = sbuf(f"res{n + 2}", [2 * SLOTS * C], F32)[:]
             for u in range(2):
-                g_part[2 + n, u] = g_late[:, 2 * u : 2 * u + 2, 2 * n * C : 2 * (n + 1) * C]
-        res = [
-            g_then_res[:, 4 * C :] if n == 1 else sbuf(f"res{n}", [2 * SLOTS * C], F32)[:] for n in range(PAIRS)
-        ]
-        h_first = sbuf("h_first", [2 * SLOTS * C], BF16)
-        h_bf = [
-            h_first[:],
-            res[0][:, : 4 * C].bitcast(BF16),
-            g_then_res[:, 2 * C : 6 * C].bitcast(BF16),
-            g_second[:].bitcast(BF16),
-        ]
-        y_bf = sbuf("y_bf", [SLOTS * J], BF16)
+                g_part[n + 2, u] = g_late[:, 2 * u : 2 * u + 2, 2 * n * C : 2 * (n + 1) * C]
+        y_bf = [sbuf(f"y_bf{n}", [2 * SLOTS * C], BF16, on=None if n else "wg_dealt") for n in range(PAIRS)]
         x_codes, h_codes, y_codes = [sbuf(f"{a}_codes", [J], U32) for a in "xhy"]
         x_sc, h_sc, y_sc = [sbuf(f"{a}_sc", [J], U8) for a in "xhy"]
 
@@ -107,10 +95,10 @@ def tile_list_sigm_mulP_kernel(
         out_rows = out_0.rearrange("(p t) j -> p t j", t=SLOTS)
         out_words = out_1[0].rearrange("p j t -> p (j t)").bitcast(I32)
 
-        def load_scale_rows(queue, first, last):
+        def load_scale_rows(first, last):
             for n in range(first, last):
                 a, q = divmod(n, 4)
-                queue.dma_start(
+                nc.sync.dma_start(
                     w_sc_raw[32 * q + 4 * a : 32 * q + 4 * a + 4, :].bitcast(I32),
                     (wg_scales, wu_scales, wd_scales)[a][0, 4 * q : 4 * q + 4, :].bitcast(I32),
                 )
@@ -120,12 +108,11 @@ def tile_list_sigm_mulP_kernel(
 
         nc.vector.memset(w_sc_raw[:].bitcast(I32), 0)
         make_identity(nc, ident[:])
-        load_scale_rows(nc.gpsimd, 0, SIDE_LOADS)
         nc.sync.dma_start(w_rows[:], wgt[0:P:8, :].rearrange("a (c x) -> a c x", x=C))
         nc.sync.dma_start(offsets[:], offs)
-        for t in (0, 1, 3):
+        for t, rows in zip((0, 1, 3), SCALE_LOADS):
             nc.sync.dma_start(x_slot[t][:], x_rows[:, t, :])
-        load_scale_rows(nc.sync, SIDE_LOADS, 12)
+            load_scale_rows(*rows)
         nc.sync.dma_start(wg_raw[:].bitcast(I32), wg_words[0].bitcast(I32))
         nc.sync.dma_start(x_slot[2][:], x_rows[:, 2, :])
         load_words(wu_raw, wu_words)
@@ -180,7 +167,7 @@ def tile_list_sigm_mulP_kernel(
         warm = sbuf("warm", [1], F32)
         nc.scalar.activation(warm[:], ident[:, 0:1], SIGMOID)
 
-        for copy, share in ((nc.scalar.copy, SPREAD[:1]), (nc.vector.tensor_copy, SPREAD[1:])):
+        for copy, share in ((nc.scalar.copy, SPREAD[0::2]), (nc.vector.tensor_copy, SPREAD[1::2])):
             turned = psum3.tile([P, P], F32, name="ysum")
             nc.tensor.transpose(turned[:], w_rows[:], ident[:])
             by_chunk = turned[:].rearrange("x (a c) -> x c a", c=CHUNKS)
@@ -189,23 +176,23 @@ def tile_list_sigm_mulP_kernel(
                     w_cols[:, j0:j1].rearrange("x (c a r) -> x c a r", a=16, r=8),
                     by_chunk[:, j0 // C : j1 // C, :].unsqueeze(3).broadcast_to([P, (j1 - j0) // C, 16, 8]),
                 )
-        for j0, j1 in SPREAD:
+        for n, (j0, j1) in enumerate(SPREAD):
             spread = psum3.tile([P, j1 - j0], F32, name="ub")
             for at in range(j0, j1, C):
                 nc.tensor.transpose(spread[:, at - j0 : at - j0 + C], w_cols[:, at : at + C], ident[:])
-            nc.scalar.copy(weight[:, j0:j1], spread[:])
+            copy = nc.vector.tensor_copy if n == 1 else nc.scalar.copy
+            copy(weight[:, j0:j1], spread[:])
 
         for j0, j1 in SPREAD:
             gather(low_picks[:, j0:j1], 0, j0, j1)
-        for j0, j1 in ((0, SECOND_CUT), (SECOND_CUT, J)):
+        for j0, j1 in ((AHEAD * C, J), (0, AHEAD * C)):
             gather(low_picks[:, J + j0 : J + j1], 1, j0, j1)
         low_slots = low_picks[:].rearrange("p (t j) -> p j t", t=2)
-        for c0, c1, part in x_parts:
+        for c0, c1, part in x_parts[-1:] + x_parts[:-1]:
             nc.scalar.copy(quads(part)[:, :, 0:2], low_slots[:, c0 * C : c1 * C, :])
         deal_narrow(nc.scalar.copy, wg_dealt[:].bitcast(U16), wg_raw[:].bitcast(U16))
-        gather(back[:, 4 * C :], 3, FRONT * C, J)
+        gather(high_picks[:, FREE * C :], 3, 0, J)
         deal_narrow(nc.vector.tensor_copy, w_sc[:], w_sc_raw[:])
-        gather(front[:, (FRONT - 1) * C :], 3, 0, FRONT * C)
 
         idle = psum3.tile([P, R], F32, name="ysum")
         for m in range(2):
@@ -232,17 +219,11 @@ def tile_list_sigm_mulP_kernel(
             slots = slice(2 * u, 2 * u + 2)
             nc.sync.dma_start(out_rows[:, slots, 2 * n * C : 2 * (n + 1) * C], results(n)[:, slots, :])
 
-        def high_blocks(c):
-            if c < FRONT:
-                return front[:].rearrange("p (b x) -> p b x", x=C), c, FRONT - 1 + c
-            return back[:].rearrange("p (b x) -> p b x", x=C), c - FRONT, 4 + c - FRONT
-
         def pick(c):
-            blocks, at = high_blocks(c)[:2]
-            gather(blocks[:, at, :], 2, c * C, (c + 1) * C)
+            gather(blocks[:, LATE_BLOCK.get(c, c), :], 2, c * C, (c + 1) * C)
 
         def round_x(c):
-            blocks, at, other = high_blocks(c)
+            at, other = LATE_BLOCK.get(c, c), FREE + c
             nc.scalar.copy(
                 quads(x_chunk(c))[:, :, 2:4], blocks[:, at : other + 1 : other - at, :].rearrange("p t x -> p x t")
             )
@@ -263,10 +244,7 @@ def tile_list_sigm_mulP_kernel(
                 product(ub[c][:, t, :], weights, WU_ROWS, t, x_codes, x_sc, slice(c * C, (c + 1) * C))
 
         def sigmoid(c):
-            if c == CHUNKS - 2:
-                sig[c] = quads(y_bf[:, : 2 * SLOTS * C].bitcast(F32))
-            else:
-                sig[c] = ring.tile([P, C, SLOTS], F32, name="sig")[:]
+            sig[c] = ring.tile([P, C, SLOTS], F32, name="sig")[:]
             nc.scalar.activation(sig[c], ga[c][:].rearrange("p t j -> p j t"), SIGMOID)
 
         def up(c):
@@ -298,33 +276,32 @@ def tile_list_sigm_mulP_kernel(
             nc.vector.tensor_tensor(results(n)[:, 2 * u : 2 * u + 2, :], ysum[n, u][:], g_part[n, u], MULT)
             store(n, u)
 
-        for c in range(FRONT - 1):
+        for c in range(FREE):
             pick(c)
             round_x(c)
         quant_x(0)
         up_gate(0)
-        pick(FRONT - 1)
-        round_x(FRONT - 1)
+        pick(FREE)
+        round_x(FREE)
         quant_x(1)
         up_gate(1)
         deal_words(nc.vector, wu_dealt, wu_raw)
         for stage in (up_value, sigmoid):
             stage(0)
             stage(1)
-        pick(5)
-        pick(6)
-        quant_x(2)
-        quant_x(3)
-        pick(7)
-        quant_x(4)
+        for c in range(2, FREE):
+            quant_x(c)
+        for c in (7, 5, 6):
+            pick(c)
+        quant_x(FREE)
         deal_words(nc.gpsimd, wd_dealt, wd_raw)
         glu(0)
         glu(1)
 
-        for c in range(FRONT, CHUNKS):
+        for c in range(AHEAD, CHUNKS):
             round_x(c)
             up(c - UB_BANKS)
-        for c in range(FRONT, CHUNKS):
+        for c in range(AHEAD, CHUNKS):
             quant_x(c)
         down(0)
 
@@ -340,20 +317,27 @@ def tile_list_sigm_mulP_kernel(
         for u in range(2):
             gate(PAIRS - 1, u)
 
-        for n in range(PAIRS):
-            last = n == PAIRS - 1
-            cut = LAST_CUT if last else C
-            second = nc.vector.tensor_copy if last else nc.scalar.copy
-            for j0, j1, copy in ((0, cut, nc.scalar.copy), (cut, 2 * C, second)):
-                dst = y_bf[:, SLOTS * (2 * n * C + j0) : SLOTS * (2 * n * C + j1)]
-                copy(
-                    dst.rearrange("p (c i t) -> p c t i", i=2, t=SLOTS),
-                    results(n)[:, :, j0:j1].rearrange("p t (c i) -> p c t i", i=2),
-                )
-            quantize(y_codes, y_sc, y_bf[:, 2 * n * SLOTS * C : 2 * (n + 1) * SLOTS * C], 2 * n, 2 * n + 2)
+        def round_y(copy, n, j0, j1):
+            copy(
+                y_bf[n][:, SLOTS * j0 : SLOTS * j1].rearrange("p (c i t) -> p c t i", i=2, t=SLOTS),
+                results(n)[:, :, j0:j1].rearrange("p t (c i) -> p c t i", i=2),
+            )
+
+        def quant_y(n):
+            quantize(y_codes, y_sc, y_bf[n][:], 2 * n, 2 * n + 2)
             for c0, c1 in WORD_STORES:
                 if c1 == 2 * n + 2:
                     nc.sync.dma_start(out_words[:, c0 * C : c1 * C], y_codes[:, c0 * C : c1 * C].bitcast(I32))
+
+        for n in range(PAIRS - 1):
+            round_y(nc.scalar.copy, n, 0, C)
+            round_y(nc.scalar.copy, n, C, 2 * C)
+        for n in range(PAIRS - 2):
+            quant_y(n)
+        round_y(nc.scalar.copy, PAIRS - 1, 0, LAST_CUT)
+        round_y(nc.vector.tensor_copy, PAIRS - 1, LAST_CUT, 2 * C)
+        quant_y(PAIRS - 2)
+        quant_y(PAIRS - 1)
 
         for q in range(4):
             queue = nc.scalar if q % 2 else nc.sync

from contextlib import ExitStack

import concourse.mybir as mybir
from concourse.masks import make_identity

K, R, N, T, J = 512, 512, 512, 2048, 1024
FLOPS = 2 * J * (2 * K * R + R * N)

F32 = mybir.dt.float32
BF16 = mybir.dt.bfloat16
I32 = mybir.dt.int32
U32 = mybir.dt.uint32
U16 = mybir.dt.uint16
U8 = mybir.dt.uint8
FP8X4 = mybir.dt.float8_e4m3fn_x4
FP4X4 = mybir.dt.float4_e2m1fn_x4
MULT = mybir.AluOpType.mult
SIGMOID = mybir.ActivationFunctionType.Sigmoid

P = 128
SLOTS = 4
C = 128
CHUNKS = J // C
PAIRS = CHUNKS // 2
LANES = 16

SPREAD = ((0, C), (C, 3 * C), (3 * C, 6 * C), (6 * C, J))
FREE = 4
LATE_BLOCK = {4: FREE, 5: FREE + 4, 6: FREE, 7: FREE + 3}
AHEAD = FREE + 1
SCALE_LOADS = ((0, 5), (5, 9), (9, 12))
WG_ROWS, WU_ROWS, WD_ROWS = 0, 4, 8
UB_BANKS = 3
SIDE_PAIRS = 2
LAST_CUT = 80
WORD_STORES = ((0, 4), (4, 6), (6, 8))


def tile_list_sigm_mulP_kernel(
    tc, xT, wgt, wg_words, wg_scales, wu_words, wu_scales, wd_words, wd_scales, g, offs, out_0, out_1, out_2
):
    nc = tc.nc
    with ExitStack() as ctx:
        keep = ctx.enter_context(tc.tile_pool(name="keep", bufs=1))
        ring = ctx.enter_context(tc.tile_pool(name="ring", bufs=CHUNKS))
        psum3 = ctx.enter_context(tc.psum_pool(name="psum3", bufs=UB_BANKS))
        psum2 = ctx.enter_context(tc.psum_pool(name="psum2", bufs=2))

        def sbuf(name, shape, dtype, on=None):
            return keep.tile([P] + shape, dtype, name=name, tag=on or name, align_bytes=64)

        offsets = keep.tile([P, J // LANES], U16, name="offsets")
        ident = sbuf("ident", [P], F32)
        w_rows = sbuf("w_rows", [C], F32)
        w_cols = sbuf("w_cols", [J], F32)
        weight = sbuf("weight", [J], F32)
        x_slot = [sbuf(f"x_slot{t}", [T], F32) for t in range(SLOTS)]
        wg_raw = sbuf("wg_raw", [2 * R], U8)
        wu_raw = sbuf("wu_raw", [R], U32)
        wd_raw = sbuf("wd_raw", [N], U32)
        w_sc_raw = sbuf("w_sc_raw", [R], U8)
        w_sc = sbuf("w_sc", [R], U8)
        wg_dealt = sbuf("wg_dealt", [2 * R], U8)

        low_picks = sbuf("low_picks", [2 * J], F32)
        high_picks = sbuf("high_picks", [(FREE + CHUNKS) * C], F32)
        blocks = high_picks[:].rearrange("p (b x) -> p b x", x=C)
        x_parts = [
            (c0, c1, sbuf(name, [(c1 - c0) * SLOTS * C], BF16)[:])
            for c0, c1, name in ((0, 1, "x_first"), (1, AHEAD, "x_mid"), (AHEAD, CHUNKS, "x_last"))
        ]
        wu_dealt = sbuf("wu_dealt", [R], U32, on="x_first")
        wd_dealt = sbuf("wd_dealt", [N], U32, on="weight")

        g_low = sbuf("g_low", [2, 4 * C], F32)
        g_late = sbuf("g_late", [SLOTS, 4 * C], F32)
        g_part = {}
        res = {}
        h_bf = {n: sbuf(f"h_bf{n}", [2 * SLOTS * C], BF16)[:] for n in range(PAIRS - SIDE_PAIRS)}
        for n in range(SIDE_PAIRS):
            shared = sbuf(f"shared{n}", [12 * C], F32)
            h_bf[n + 2] = shared[:, : 4 * C].bitcast(BF16)
            res[n] = shared[:, 4 * C :]
            g_part[n, 1] = shared[:, 3 * C // 2 : 11 * C // 2].rearrange("p (t j) -> p t j", t=2)
            g_part[n, 0] = g_low[:, :, 2 * n * C : 2 * (n + 1) * C]
            res[n + 2] = sbuf(f"res{n + 2}", [2 * SLOTS * C], F32)[:]
            for u in range(2):
                g_part[n + 2, u] = g_late[:, 2 * u : 2 * u + 2, 2 * n * C : 2 * (n + 1) * C]
        y_bf = [sbuf(f"y_bf{n}", [2 * SLOTS * C], BF16, on=None if n else "wg_dealt") for n in range(PAIRS)]
        x_codes, h_codes, y_codes = [sbuf(f"{a}_codes", [J], U32) for a in "xhy"]
        x_sc, h_sc, y_sc = [sbuf(f"{a}_sc", [J], U8) for a in "xhy"]

        x_rows = xT.rearrange("(p t) i -> p t i", t=SLOTS)
        g_rows = g.rearrange("(p t) j -> p t j", t=SLOTS)
        out_rows = out_0.rearrange("(p t) j -> p t j", t=SLOTS)
        out_words = out_1[0].rearrange("p j t -> p (j t)").bitcast(I32)

        def load_scale_rows(first, last):
            for n in range(first, last):
                a, q = divmod(n, 4)
                nc.sync.dma_start(
                    w_sc_raw[32 * q + 4 * a : 32 * q + 4 * a + 4, :].bitcast(I32),
                    (wg_scales, wu_scales, wd_scales)[a][0, 4 * q : 4 * q + 4, :].bitcast(I32),
                )

        def load_words(dst, words):
            nc.sync.dma_start(dst[:].bitcast(I32), words[0].rearrange("p n t -> p (n t)").bitcast(I32))

        nc.vector.memset(w_sc_raw[:].bitcast(I32), 0)
        make_identity(nc, ident[:])
        nc.sync.dma_start(w_rows[:], wgt[0:P:8, :].rearrange("a (c x) -> a c x", x=C))
        nc.sync.dma_start(offsets[:], offs)
        for t, rows in zip((0, 1, 3), SCALE_LOADS):
            nc.sync.dma_start(x_slot[t][:], x_rows[:, t, :])
            load_scale_rows(*rows)
        nc.sync.dma_start(wg_raw[:].bitcast(I32), wg_words[0].bitcast(I32))
        nc.sync.dma_start(x_slot[2][:], x_rows[:, 2, :])
        load_words(wu_raw, wu_words)
        load_words(wd_raw, wd_words)
        nc.sync.dma_start(g_part[0, 1], g_rows[:, 2:4, : 2 * C])
        nc.sync.dma_start(g_low[:], g_rows[:, 0:2, : 4 * C])
        nc.sync.dma_start(g_part[1, 1], g_rows[:, 2:4, 2 * C : 4 * C])
        nc.sync.dma_start(g_late[:], g_rows[:, :, 4 * C :])

        def gather(dst, t, j0, j1):
            nc.vector.tensor_tensor(
                dst, x_slot[t][:].indirect(offsets[:, j0 // LANES : j1 // LANES]), weight[:, j0:j1], MULT
            )

        def deal_narrow(copy, dst, src):
            copy(dst.rearrange("p (t m) -> p t m", t=SLOTS), src.rearrange("p (m t) -> p t m", t=SLOTS))

        def deal_words(engine, dst, src):
            engine.tensor_copy(
                dst[:].bitcast(I32).rearrange("p (t m i) -> p m t i", t=SLOTS, i=4),
                src[:].bitcast(I32).rearrange("p (m i t) -> p m t i", t=SLOTS, i=4),
            )

        def quantize(codes, scales, src, c0, c1):
            nc.vector.quantize_mx(
                out=codes[:, c0 * C : c1 * C].bitcast(FP8X4),
                scales=scales[:, c0 * C : c1 * C],
                in_=src,
            )

        def product(acc, weights, scale_rows, t, codes, scales, cols):
            nc.tensor.matmul_mx(
                out=acc,
                lhsT=weights,
                lhsT_scale=w_sc[scale_rows:, t * P : (t + 1) * P],
                rhs=codes[:, cols].bitcast(FP8X4),
                rhs_scale=scales[:, cols],
                start=True,
                stop=True,
            )

        def wide(c):
            return slice(SLOTS * c * C, SLOTS * (c + 1) * C)

        def x_chunk(c):
            first, held = [(c0, part) for c0, c1, part in x_parts if c0 <= c < c1][0]
            return held[:, wide(c - first)]

        def quads(ap):
            return ap.rearrange("p (j t) -> p j t", t=SLOTS)

        warm = sbuf("warm", [1], F32)
        nc.scalar.activation(warm[:], ident[:, 0:1], SIGMOID)

        for copy, share in ((nc.scalar.copy, SPREAD[0::2]), (nc.vector.tensor_copy, SPREAD[1::2])):
            turned = psum3.tile([P, P], F32, name="ysum")
            nc.tensor.transpose(turned[:], w_rows[:], ident[:])
            by_chunk = turned[:].rearrange("x (a c) -> x c a", c=CHUNKS)
            for j0, j1 in share:
                copy(
                    w_cols[:, j0:j1].rearrange("x (c a r) -> x c a r", a=16, r=8),
                    by_chunk[:, j0 // C : j1 // C, :].unsqueeze(3).broadcast_to([P, (j1 - j0) // C, 16, 8]),
                )
        for n, (j0, j1) in enumerate(SPREAD):
            spread = psum3.tile([P, j1 - j0], F32, name="ub")
            for at in range(j0, j1, C):
                nc.tensor.transpose(spread[:, at - j0 : at - j0 + C], w_cols[:, at : at + C], ident[:])
            copy = nc.vector.tensor_copy if n == 1 else nc.scalar.copy
            copy(weight[:, j0:j1], spread[:])

        for j0, j1 in SPREAD:
            gather(low_picks[:, j0:j1], 0, j0, j1)
        for j0, j1 in ((AHEAD * C, J), (0, AHEAD * C)):
            gather(low_picks[:, J + j0 : J + j1], 1, j0, j1)
        low_slots = low_picks[:].rearrange("p (t j) -> p j t", t=2)
        for c0, c1, part in x_parts[-1:] + x_parts[:-1]:
            nc.scalar.copy(quads(part)[:, :, 0:2], low_slots[:, c0 * C : c1 * C, :])
        deal_narrow(nc.scalar.copy, wg_dealt[:].bitcast(U16), wg_raw[:].bitcast(U16))
        gather(high_picks[:, FREE * C :], 3, 0, J)
        deal_narrow(nc.vector.tensor_copy, w_sc[:], w_sc_raw[:])

        idle = psum3.tile([P, R], F32, name="ysum")
        for m in range(2):
            nc.tensor.matmul_mx(
                out=idle[:],
                lhsT=wu_raw[:, m * P : (m + 1) * P].bitcast(FP8X4),
                lhsT_scale=w_sc[WU_ROWS:, m * P : (m + 1) * P],
                rhs=wu_raw[:].bitcast(FP8X4),
                rhs_scale=w_sc[WU_ROWS:, :],
                start=True,
                stop=True,
            )

        ga = {}
        sig = {}
        ub = {}
        ysum = {}
        y_copy = {}

        def results(n):
            return res[n].rearrange("p (t j) -> p t j", t=SLOTS)

        def store(n, u):
            slots = slice(2 * u, 2 * u + 2)
            nc.sync.dma_start(out_rows[:, slots, 2 * n * C : 2 * (n + 1) * C], results(n)[:, slots, :])

        def pick(c):
            gather(blocks[:, LATE_BLOCK.get(c, c), :], 2, c * C, (c + 1) * C)

        def round_x(c):
            at, other = LATE_BLOCK.get(c, c), FREE + c
            nc.scalar.copy(
                quads(x_chunk(c))[:, :, 2:4], blocks[:, at : other + 1 : other - at, :].rearrange("p t x -> p x t")
            )

        def quant_x(c):
            quantize(x_codes, x_sc, x_chunk(c), c, c + 1)

        def up_gate(c):
            ga[c] = psum2.tile([P, SLOTS, C], F32, name="ga")
            for t in range(SLOTS):
                weights = wg_dealt[:, 2 * t * P : 2 * (t + 1) * P].bitcast(FP4X4)
                product(ga[c][:, t, :], weights, WG_ROWS, t, x_codes, x_sc, slice(c * C, (c + 1) * C))

        def up_value(c):
            ub[c] = psum3.tile([P, SLOTS, C], F32, name="ub")
            for t in range(SLOTS):
                weights = wu_dealt[:, t * P : (t + 1) * P].bitcast(FP8X4)
                product(ub[c][:, t, :], weights, WU_ROWS, t, x_codes, x_sc, slice(c * C, (c + 1) * C))

        def sigmoid(c):
            sig[c] = ring.tile([P, C, SLOTS], F32, name="sig")[:]
            nc.scalar.activation(sig[c], ga[c][:].rearrange("p t j -> p j t"), SIGMOID)

        def up(c):
            up_gate(c)
            up_value(c)
            sigmoid(c)

        def glu(c):
            nc.vector.tensor_tensor(
                quads(h_bf[c // 2][:, wide(c % 2)]), ub[c][:].rearrange("p t j -> p j t"), sig[c], MULT
            )

        def down(n):
            quantize(h_codes, h_sc, h_bf[n], 2 * n, 2 * n + 2)
            cols = slice(2 * n * C, 2 * (n + 1) * C)
            for u in (1, 0) if n < SIDE_PAIRS else (0, 1):
                ysum[n, u] = psum3.tile([P, 2, 2 * C], F32, name="ysum")
                for t in (2 * u, 2 * u + 1):
                    weights = wd_dealt[:, t * P : (t + 1) * P].bitcast(FP8X4)
                    product(ysum[n, u][:, t % 2, :], weights, WD_ROWS, t, h_codes, h_sc, cols)
            if 1 <= n <= SIDE_PAIRS:
                nc.gpsimd.tensor_tensor(results(n - 1)[:, 0:2, :], y_copy[n - 1][:], g_part[n - 1, 0], MULT)
                store(n - 1, 0)
            if n < SIDE_PAIRS:
                y_copy[n] = sbuf(f"y_copy{n}", [2, 2 * C], F32)
                nc.scalar.copy(y_copy[n][:], ysum[n, 0][:])

        def gate(n, u):
            nc.vector.tensor_tensor(results(n)[:, 2 * u : 2 * u + 2, :], ysum[n, u][:], g_part[n, u], MULT)
            store(n, u)

        for c in range(FREE):
            pick(c)
            round_x(c)
        quant_x(0)
        up_gate(0)
        pick(FREE)
        round_x(FREE)
        quant_x(1)
        up_gate(1)
        deal_words(nc.vector, wu_dealt, wu_raw)
        for stage in (up_value, sigmoid):
            stage(0)
            stage(1)
        for c in range(2, FREE):
            quant_x(c)
        for c in (7, 5, 6):
            pick(c)
        quant_x(FREE)
        deal_words(nc.gpsimd, wd_dealt, wd_raw)
        glu(0)
        glu(1)

        for c in range(AHEAD, CHUNKS):
            round_x(c)
            up(c - UB_BANKS)
        for c in range(AHEAD, CHUNKS):
            quant_x(c)
        down(0)

        for c in range(2, CHUNKS):
            glu(c)
            if c + UB_BANKS < CHUNKS:
                up(c + UB_BANKS)
            if c % 2:
                n = c // 2
                gate(n - 1, 1 if n - 1 < SIDE_PAIRS else 0)
                down(n)
        gate(PAIRS - 2, 1)
        for u in range(2):
            gate(PAIRS - 1, u)

        def round_y(copy, n, j0, j1):
            copy(
                y_bf[n][:, SLOTS * j0 : SLOTS * j1].rearrange("p (c i t) -> p c t i", i=2, t=SLOTS),
                results(n)[:, :, j0:j1].rearrange("p t (c i) -> p c t i", i=2),
            )

        def quant_y(n):
            quantize(y_codes, y_sc, y_bf[n][:], 2 * n, 2 * n + 2)
            for c0, c1 in WORD_STORES:
                if c1 == 2 * n + 2:
                    nc.sync.dma_start(out_words[:, c0 * C : c1 * C], y_codes[:, c0 * C : c1 * C].bitcast(I32))

        for n in range(PAIRS - 1):
            round_y(nc.scalar.copy, n, 0, C)
            round_y(nc.scalar.copy, n, C, 2 * C)
        for n in range(PAIRS - 2):
            quant_y(n)
        round_y(nc.scalar.copy, PAIRS - 1, 0, LAST_CUT)
        round_y(nc.vector.tensor_copy, PAIRS - 1, LAST_CUT, 2 * C)
        quant_y(PAIRS - 2)
        quant_y(PAIRS - 1)

        for q in range(4):
            queue = nc.scalar if q % 2 else nc.sync
            queue.dma_start(
                out_2[0, 4 * q : 4 * q + 4, :].bitcast(I32), y_sc[32 * q : 32 * q + 4, :].bitcast(I32)
            )
